import numpy as np
import ml_dtypes


def mxq(x, axis, fmt="e4m3"):
    dtype, down = {"e4m3": (ml_dtypes.float8_e4m3fn, 7), "e5m2": (ml_dtypes.float8_e5m2, 14)}[fmt]
    v = np.moveaxis(np.asarray(x, np.float32).astype(ml_dtypes.bfloat16).astype(np.float64), axis, -1)
    blocks = v.reshape(v.shape[:-1] + (-1, 32))
    amax = np.abs(blocks).max(-1, keepdims=True)
    byte = np.maximum(np.where(amax > 0, np.frexp(amax)[1] - 1 + 127, 0) - down, 1)
    scale = np.exp2(byte - 127.0)
    codes = (blocks / scale).astype(np.float32).astype(dtype).astype(np.float64)
    return np.moveaxis((codes * scale).reshape(v.shape), -1, axis)


WIDE = False


def mx_kscale(k):
    if not WIDE:
        return np.ones(k)
    levels = np.array([10, -10, 5, -5, 0])
    if k % 512:
        return np.exp2(np.random.permutation(np.resize(levels, k // 32))).repeat(32)
    a = np.empty((k // 512, 16))
    for p in range(k // 512):
        a[p, :8] = np.random.permutation(np.resize(levels, 8))
        for g in range(8):
            far = levels[np.abs(levels - a[p, g]) >= 10]
            a[p, g + 8] = far[np.random.randint(len(far))]
    return np.exp2(a.ravel()).repeat(32)


def f64(x):
    return np.asarray(x).astype(np.float64)


def striped(idx):
    return np.tile(idx.reshape(-1, 16).T, (8, 1)).astype(np.uint16)


def unstriped(offs):
    return offs[:16].T.reshape(-1).astype(np.int64)


def pack_weight(w):
    k, n = w.shape
    w = f64(np.asarray(w, np.float32).astype(ml_dtypes.bfloat16)).reshape(k // 32, 32, n)
    amax = np.abs(w).max(1)
    byte = np.clip(np.where(amax > 0, np.frexp(amax)[1] - 1 + 127 - 7, 1), 1, 254)
    scaled = (w * np.exp2(127.0 - byte)[:, None, :]).reshape(k, n).astype(np.float32)
    words = np.ascontiguousarray(scaled.reshape(k // 512, 128, 4, n).transpose(0, 1, 3, 2)).astype(ml_dtypes.float8_e4m3fn).view(np.uint8)
    return words, np.ascontiguousarray(byte.astype(np.uint8).reshape(k // 512, 16, n))


def unpack_weight(words, scales):
    g, p, n, _ = words.shape
    vals = np.ascontiguousarray(words).view(ml_dtypes.float8_e4m3fn).astype(np.float64) * np.repeat(np.exp2(scales.astype(np.float64) - 127.0), 8, axis=1)[..., None]
    return vals.transpose(0, 1, 3, 2).reshape(g * 512, n)


def relu(v):
    return np.maximum(v, 0.0)


K, T, S, V, H, N = 1024, 2048, 1024, 512, 512, 256


def setup_inputs():
    n = np.random.standard_normal
    s = mx_kscale(K)[:, None]
    u = mx_kscale(H)
    packed_w2 = pack_weight(n((H, N)) / np.sqrt(2 * H) / u[:, None])
    packed_w3 = pack_weight(n((H, N)) / np.sqrt(2 * H) / u[:, None])
    return {
        "xT": (n((K, T)) * s).astype(np.float32),
        "w1": (n((K, H)) / np.sqrt(K) / s * u).astype(np.float32),
        "w2_words": packed_w2[0],
        "w2_scales": packed_w2[1],
        "w3_words": packed_w3[0],
        "w3_scales": packed_w3[1],
        "offs": striped(np.random.permutation(T)[:S]),
    }


def reference(xT, w1, w2_words, w2_scales, w3_words, w3_scales, offs):
    xq = mxq(f64(xT)[:, unstriped(offs)], 0, "e4m3")
    h = relu(mxq(f64(w1), 0, "e4m3").T @ xq)
    low = 0.5 * (h[:, :V] + h[:, V:2 * V])
    high = 0.5 * (h[:, :V] - h[:, V:2 * V])
    return unpack_weight(w2_words, w2_scales).T @ mxq(low, 0, "e4m3") + unpack_weight(w3_words, w3_scales).T @ mxq(high, 0, "e4m3")

@@ -1,0 +1,212 @@
+from contextlib import ExitStack
+
+import concourse.mybir as mybir
+
+K, T, S, V, H, N = 1024, 2048, 1024, 512, 512, 256
+FLOPS = 2 * K * H * S + 2 * 2 * H * N * V
+
+F32 = mybir.dt.float32
+BF16 = mybir.dt.bfloat16
+U32 = mybir.dt.uint32
+I32 = mybir.dt.int32
+U16 = mybir.dt.uint16
+U8 = mybir.dt.uint8
+FP8X4 = mybir.dt.float8_e4m3fn_x4
+ACT = mybir.ActivationFunctionType
+ALU = mybir.AluOpType
+
+P = 128
+PACK = 4
+K_PASS = P * PACK
+PASSES = K // K_PASS
+CHUNK = 128
+GROUP = 256
+LIST_COL = 16
+
+X_LOADS = [[1024, 1024], [1024, 512, 256, 256]]
+W_HALF = H // 2
+
+
+def tile_picked_haar_relu_e_kernel(
+    tc, xT, w1, w2_words, w2_scales, w3_words, w3_scales, offs, out
+):
+    nc = tc.nc
+    with ExitStack() as ctx:
+        keep = ctx.enter_context(tc.tile_pool(name="keep", bufs=1))
+        psum = ctx.enter_context(tc.psum_pool(name="psum", bufs=1))
+
+        offsets = keep.tile([P, S // LIST_COL], U16, name="offsets")
+        x_bytes = keep.tile([P, T], U8, name="x_bytes", align_bytes=64)
+        band_scales = keep.tile([P, 2 * N], U8, name="band_scales", align_bytes=64)
+        nc.gpsimd.memset(x_bytes[:].bitcast(I32), 0)
+        nc.gpsimd.memset(band_scales[:].bitcast(I32), 0)
+        for band, scales in enumerate((w2_scales, w3_scales)):
+            for q in range(4):
+                nc.gpsimd.dma_start(
+                    out=band_scales[32 * q : 32 * q + 4, band * N : (band + 1) * N].bitcast(I32),
+                    in_=scales[0, 4 * q : 4 * q + 4, :].bitcast(I32),
+                )
+
+        x_raw = []
+        for z in range(PASSES):
+            t0 = 0
+            for width in X_LOADS[z]:
+                raw = keep.tile([P, PACK, width], F32, name="x_raw_%d_%d" % (z, t0))
+                rows = xT[z * K_PASS : (z + 1) * K_PASS, t0 : t0 + width]
+                nc.sync.dma_start(out=raw[:], in_=rows.rearrange("(p j) t -> p j t", j=PACK))
+                x_raw.append((z, t0, width, raw))
+                if z == 0 and t0 == 0:
+                    nc.sync.dma_start(offsets[:], offs)
+                t0 = t0 + width
+        w_raw = {}
+        for z in range(PASSES):
+            for half in range(2):
+                raw = keep.tile([P, PACK, W_HALF], F32, name="w_raw_%d_%d" % (z, half))
+                rows = w1[z * K_PASS : (z + 1) * K_PASS, half * W_HALF : (half + 1) * W_HALF]
+                nc.sync.dma_start(out=raw[:], in_=rows.rearrange("(p j) c -> p j c", j=PACK))
+                w_raw[z, half] = raw
+        band_words = []
+        for band, words in enumerate((w2_words, w3_words)):
+            codes = keep.tile([P, N], U32, name="band_words_%d" % band, align_bytes=64)
+            nc.sync.dma_start(
+                out=codes[:].bitcast(I32),
+                in_=words[0].rearrange("p n t -> p (n t)").bitcast(I32),
+            )
+            band_words.append(codes)
+
+        x_words = [keep.tile([P, T], U32, name="x_words_%d" % z, align_bytes=64) for z in range(PASSES)]
+        picked_words = {}
+        unit = 0
+        for z, t0, width, raw in x_raw:
+            step = 128 if width == 256 else 256
+            for a in range(0, width, step):
+                grouped = keep.tile([P, step * PACK], BF16, name="x_bf16_%d_%d" % (z, t0 + a), align_bytes=64)
+                dst = grouped[:].rearrange("p (c i j) -> p c j i", i=4, j=PACK)
+                src = raw[:, :, a : a + step].rearrange("p j (c i) -> p c j i", i=4)
+                if unit % 2 == 0:
+                    nc.scalar.activation(out=dst, in_=src, func=ACT.Copy)
+                else:
+                    nc.vector.tensor_copy(out=dst, in_=src)
+                unit = unit + 1
+                cols = slice(t0 + a, t0 + a + step)
+                nc.vector.quantize_mx(
+                    out=x_words[z][:, cols].bitcast(FP8X4),
+                    scales=x_bytes[4 * z : P, cols],
+                    in_=grouped[:],
+                )
+            if z == 0 and t0 + width == T:
+                first = keep.tile([P, S], U32, name="picked_words_0", align_bytes=64)
+                nc.vector.tensor_copy(out=first[:], in_=x_words[0][:].indirect(offsets[:]))
+                for g in range(S // GROUP):
+                    picked_words[0, g] = first[:, g * GROUP : (g + 1) * GROUP]
+
+        picked_bytes = {}
+
+        def piece(g):
+            return offsets[:, g * GROUP // LIST_COL : (g + 1) * GROUP // LIST_COL]
+
+        def gather_bytes(groups, tag):
+            by = keep.tile([P, 2 * GROUP], U8, name="picked_bytes_%d" % groups[0], tag=tag, align_bytes=64)
+            for i, g in enumerate(groups):
+                picked_bytes[g] = by[:, i * GROUP : (i + 1) * GROUP]
+                nc.vector.tensor_copy(out=picked_bytes[g], in_=x_bytes[:].indirect(piece(g)))
+
+        def gather_words(groups, tag):
+            wo = keep.tile([P, 2 * GROUP], U32, name="picked_words_1_%d" % groups[0], tag=tag, align_bytes=64)
+            for i, g in enumerate(groups):
+                picked_words[1, g] = wo[:, i * GROUP : (i + 1) * GROUP]
+                nc.vector.tensor_copy(out=picked_words[1, g], in_=x_words[1][:].indirect(piece(g)))
+
+        w_words, w_scales = {}, {}
+
+        def quantise_w1(z):
+            grouped = keep.tile([P, H * PACK], BF16, name="w_bf16_%d" % z, tag="w_bf16_%d" % z, align_bytes=64)
+            view = grouped[:].rearrange("p (t m j) -> p m t j", t=PACK, j=PACK)
+            for half in range(2):
+                nc.scalar.activation(
+                    out=view[:, half * 64 : (half + 1) * 64],
+                    in_=w_raw[z, half][:].rearrange("p j (m t) -> p m t j", t=PACK),
+                    func=ACT.Copy,
+                    scale=0.5,
+                )
+            w_words[z] = keep.tile([P, H], U32, name="w_words_%d" % z, align_bytes=64)
+            w_scales[z] = keep.tile([P, H], U8, name="w_scales_%d" % z, align_bytes=64)
+            nc.vector.quantize_mx(out=w_words[z][:].bitcast(FP8X4), scales=w_scales[z][:], in_=grouped[:])
+
+        banks = {}
+
+        def layer_pass(z, e):
+            if z == 0:
+                banks[e] = psum.tile([P, PACK, CHUNK], F32, name="bank_%d" % e, tag="bank_%d" % e)
+            g, cols = e // 2, slice((e % 2) * CHUNK, (e % 2 + 1) * CHUNK)
+            for t in range(PACK):
+                m = slice(t * P, (t + 1) * P)
+                nc.tensor.matmul_mx(
+                    out=banks[e][:, t, :],
+                    lhsT=w_words[z][:, m].bitcast(FP8X4),
+                    lhsT_scale=w_scales[z][:, m],
+                    rhs=picked_words[z, g][:, cols].bitcast(FP8X4),
+                    rhs_scale=picked_bytes[g][4 * z : P, cols],
+                    start=(z == 0 and t == 0),
+                    stop=(z == PASSES - 1 and t == PACK - 1),
+                )
+
+        bands = {}
+
+        def haar(c):
+            second = keep.tile([P, CHUNK, PACK], F32, name="second_%d" % c)
+            nc.scalar.activation(out=second[:], in_=banks[4 + c][:].rearrange("p t n -> p n t"), func=ACT.Relu)
+            bands[c] = keep.tile([P, 2, CHUNK, PACK], BF16, name="bands_%d" % c, align_bytes=64)
+            for band, op in enumerate((ALU.add, ALU.subtract)):
+                nc.vector.scalar_tensor_tensor(
+                    out=bands[c][:, band],
+                    in0=banks[c][:].rearrange("p t n -> p n t"),
+                    scalar=0.0,
+                    in1=second[:],
+                    op0=ALU.max,
+                    op1=op,
+                )
+
+        out_view = out.rearrange("(h m) v -> m h v", m=P)
+
+        def finish(c):
+            words = keep.tile([P, 2 * CHUNK], U32, name="haar_words_%d" % c, align_bytes=64)
+            scales = keep.tile([P, 2 * CHUNK], U8, name="haar_scales_%d" % c, align_bytes=64)
+            nc.vector.quantize_mx(
+                out=words[:].bitcast(FP8X4), scales=scales[:], in_=bands[c][:].rearrange("p b n t -> p (b n t)")
+            )
+            acc = psum.tile([P, 2, CHUNK], F32, name="acc_%d" % c, tag="bank_%d" % (4 + c))
+            for h in range(2):
+                for band in range(2):
+                    cols = slice(band * CHUNK, (band + 1) * CHUNK)
+                    nc.tensor.matmul_mx(
+                        out=acc[:, h, :],
+                        lhsT=band_words[band][:, h * P : (h + 1) * P].bitcast(FP8X4),
+                        lhsT_scale=band_scales[:, band * N + h * P : band * N + (h + 1) * P],
+                        rhs=words[:, cols].bitcast(FP8X4),
+                        rhs_scale=scales[:, cols],
+                        start=(band == 0),
+                        stop=(band == 1),
+                    )
+            result = keep.tile([P, 2, CHUNK], F32, name="result_%d" % c)
+            nc.scalar.activation(out=result[:], in_=acc[:], func=ACT.Copy)
+            nc.sync.dma_start(out=out_view[:, :, c * CHUNK : (c + 1) * CHUNK], in_=result[:])
+
+        gather_bytes((2, 0), "early_bytes")
+        gather_words((2, 0), "early_words")
+        quantise_w1(0)
+        for e in (4, 0, 5, 1):
+            layer_pass(0, e)
+        gather_words((3, 1), "w_bf16_0")
+        quantise_w1(1)
+        for e in (4, 0, 5, 1):
+            layer_pass(1, e)
+        gather_bytes((3, 1), "w_bf16_1")
+        for e in (6, 2, 7, 3):
+            for z in range(PASSES):
+                layer_pass(z, e)
+        haar(0)
+        for c in range(1, 4):
+            haar(c)
+            finish(c - 1)
+        finish(3)

@@ -24,7 +24,7 @@ GROUP = 256
 LIST_COL = 16
 
 X_LOADS = [[1024, 1024], [1024, 512, 256, 256]]
-W_HALF = H // 2
+W_SCALAR = 96
 
 
 def tile_picked_haar_relu_e_kernel(
@@ -58,13 +58,12 @@ def tile_picked_haar_relu_e_kernel(
                 if z == 0 and t0 == 0:
                     nc.sync.dma_start(offsets[:], offs)
                 t0 = t0 + width
-        w_raw = {}
+        w_raw = []
         for z in range(PASSES):
-            for half in range(2):
-                raw = keep.tile([P, PACK, W_HALF], F32, name="w_raw_%d_%d" % (z, half))
-                rows = w1[z * K_PASS : (z + 1) * K_PASS, half * W_HALF : (half + 1) * W_HALF]
-                nc.sync.dma_start(out=raw[:], in_=rows.rearrange("(p j) c -> p j c", j=PACK))
-                w_raw[z, half] = raw
+            raw = keep.tile([P, PACK, H], F32, name="w_raw_%d" % z, tag="w_raw_%d" % z, align_bytes=64)
+            rows = w1[z * K_PASS : (z + 1) * K_PASS, :]
+            nc.sync.dma_start(out=raw[:], in_=rows.rearrange("(p j) c -> p j c", j=PACK))
+            w_raw.append(raw)
         band_words = []
         for band, words in enumerate((w2_words, w3_words)):
             codes = keep.tile([P, N], U32, name="band_words_%d" % band, align_bytes=64)
@@ -76,18 +75,16 @@ def tile_picked_haar_relu_e_kernel(
 
         x_words = [keep.tile([P, T], U32, name="x_words_%d" % z, align_bytes=64) for z in range(PASSES)]
         picked_words = {}
-        unit = 0
         for z, t0, width, raw in x_raw:
-            step = 128 if width == 256 else 256
+            step = min(256, width // 2)
             for a in range(0, width, step):
                 grouped = keep.tile([P, step * PACK], BF16, name="x_bf16_%d_%d" % (z, t0 + a), align_bytes=64)
                 dst = grouped[:].rearrange("p (c i j) -> p c j i", i=4, j=PACK)
                 src = raw[:, :, a : a + step].rearrange("p j (c i) -> p c j i", i=4)
-                if unit % 2 == 0:
-                    nc.scalar.activation(out=dst, in_=src, func=ACT.Copy)
-                else:
+                if (a // step) % 2 == 0:
                     nc.vector.tensor_copy(out=dst, in_=src)
-                unit = unit + 1
+                else:
+                    nc.scalar.activation(out=dst, in_=src, func=ACT.Copy)
                 cols = slice(t0 + a, t0 + a + step)
                 nc.vector.quantize_mx(
                     out=x_words[z][:, cols].bitcast(FP8X4),
@@ -120,15 +117,13 @@ def tile_picked_haar_relu_e_kernel(
         w_words, w_scales = {}, {}
 
         def quantise_w1(z):
-            grouped = keep.tile([P, H * PACK], BF16, name="w_bf16_%d" % z, tag="w_bf16_%d" % z, align_bytes=64)
-            view = grouped[:].rearrange("p (t m j) -> p m t j", t=PACK, j=PACK)
-            for half in range(2):
-                nc.scalar.activation(
-                    out=view[:, half * 64 : (half + 1) * 64],
-                    in_=w_raw[z, half][:].rearrange("p j (m t) -> p m t j", t=PACK),
-                    func=ACT.Copy,
-                    scale=0.5,
-                )
+            grouped = keep.tile([P, H * PACK], BF16, name="w_bf16_%d" % z, tag="w_bf16", align_bytes=64)
+            dst = grouped[:].rearrange("p (t m j) -> p m j t", t=PACK, j=PACK)
+            src = w_raw[z][:].rearrange("p j (m t) -> p m j t", t=PACK)
+            nc.scalar.activation(out=dst[:, :W_SCALAR], in_=src[:, :W_SCALAR], func=ACT.Copy, scale=0.5)
+            nc.vector.tensor_scalar(
+                out=dst[:, W_SCALAR:], in0=src[:, W_SCALAR:], scalar1=0.5, scalar2=None, op0=ALU.mult
+            )
             w_words[z] = keep.tile([P, H], U32, name="w_words_%d" % z, align_bytes=64)
             w_scales[z] = keep.tile([P, H], U8, name="w_scales_%d" % z, align_bytes=64)
             nc.vector.quantize_mx(out=w_words[z][:].bitcast(FP8X4), scales=w_scales[z][:], in_=grouped[:])
@@ -172,9 +167,15 @@ def tile_picked_haar_relu_e_kernel(
         def finish(c):
             words = keep.tile([P, 2 * CHUNK], U32, name="haar_words_%d" % c, align_bytes=64)
             scales = keep.tile([P, 2 * CHUNK], U8, name="haar_scales_%d" % c, align_bytes=64)
-            nc.vector.quantize_mx(
-                out=words[:].bitcast(FP8X4), scales=scales[:], in_=bands[c][:].rearrange("p b n t -> p (b n t)")
-            )
+            both = bands[c][:].rearrange("p b n t -> p (b n t)")
+            parts = 2 if c == 3 else 1
+            for i in range(parts):
+                w = 2 * CHUNK // parts
+                nc.vector.quantize_mx(
+                    out=words[:, i * w : (i + 1) * w].bitcast(FP8X4),
+                    scales=scales[:, i * w : (i + 1) * w],
+                    in_=both[:, i * w * PACK : (i + 1) * w * PACK],
+                )
             acc = psum.tile([P, 2, CHUNK], F32, name="acc_%d" % c, tag="bank_%d" % (4 + c))
             for h in range(2):
                 for band in range(2):
@@ -197,11 +198,11 @@ def tile_picked_haar_relu_e_kernel(
         quantise_w1(0)
         for e in (4, 0, 5, 1):
             layer_pass(0, e)
-        gather_words((3, 1), "w_bf16_0")
+        gather_words((3, 1), "w_raw_0")
         quantise_w1(1)
         for e in (4, 0, 5, 1):
             layer_pass(1, e)
-        gather_bytes((3, 1), "w_bf16_1")
+        gather_bytes((3, 1), "w_bf16")
         for e in (6, 2, 7, 3):
             for z in range(PASSES):
                 layer_pass(z, e)

@@ -24,7 +24,7 @@ GROUP = 256
 LIST_COL = 16
 
 X_LOADS = [[1024, 1024], [1024, 512, 256, 256]]
-W_SCALAR = 96
+W_SCALAR = [128, 72]
 
 
 def tile_picked_haar_relu_e_kernel(
@@ -40,13 +40,6 @@ def tile_picked_haar_relu_e_kernel(
         band_scales = keep.tile([P, 2 * N], U8, name="band_scales", align_bytes=64)
         nc.gpsimd.memset(x_bytes[:].bitcast(I32), 0)
         nc.gpsimd.memset(band_scales[:].bitcast(I32), 0)
-        for band, scales in enumerate((w2_scales, w3_scales)):
-            for q in range(4):
-                nc.gpsimd.dma_start(
-                    out=band_scales[32 * q : 32 * q + 4, band * N : (band + 1) * N].bitcast(I32),
-                    in_=scales[0, 4 * q : 4 * q + 4, :].bitcast(I32),
-                )
-
         x_raw = []
         for z in range(PASSES):
             t0 = 0
@@ -72,6 +65,13 @@ def tile_picked_haar_relu_e_kernel(
                 in_=words[0].rearrange("p n t -> p (n t)").bitcast(I32),
             )
             band_words.append(codes)
+
+        for band, scales in enumerate((w2_scales, w3_scales)):
+            for q in range(4):
+                nc.sync.dma_start(
+                    out=band_scales[32 * q : 32 * q + 4, band * N : (band + 1) * N].bitcast(I32),
+                    in_=scales[0, 4 * q : 4 * q + 4, :].bitcast(I32),
+                )
 
         x_words = [keep.tile([P, T], U32, name="x_words_%d" % z, align_bytes=64) for z in range(PASSES)]
         picked_words = {}
@@ -117,21 +117,28 @@ def tile_picked_haar_relu_e_kernel(
         w_words, w_scales = {}, {}
 
         def quantise_w1(z):
-            grouped = keep.tile([P, H * PACK], BF16, name="w_bf16_%d" % z, tag="w_bf16", align_bytes=64)
+            grouped = keep.tile([P, H * PACK], BF16, name="w_bf16_%d" % z, tag="w_bf16_%d" % z, align_bytes=64)
             dst = grouped[:].rearrange("p (t m j) -> p m j t", t=PACK, j=PACK)
             src = w_raw[z][:].rearrange("p j (m t) -> p m j t", t=PACK)
-            nc.scalar.activation(out=dst[:, :W_SCALAR], in_=src[:, :W_SCALAR], func=ACT.Copy, scale=0.5)
-            nc.vector.tensor_scalar(
-                out=dst[:, W_SCALAR:], in0=src[:, W_SCALAR:], scalar1=0.5, scalar2=None, op0=ALU.mult
-            )
+            cut = W_SCALAR[z]
+            nc.scalar.activation(out=dst[:, :cut], in_=src[:, :cut], func=ACT.Copy, scale=0.5)
+            if cut < P:
+                nc.vector.tensor_scalar(out=dst[:, cut:], in0=src[:, cut:], scalar1=0.5, scalar2=None, op0=ALU.mult)
             w_words[z] = keep.tile([P, H], U32, name="w_words_%d" % z, align_bytes=64)
             w_scales[z] = keep.tile([P, H], U8, name="w_scales_%d" % z, align_bytes=64)
-            nc.vector.quantize_mx(out=w_words[z][:].bitcast(FP8X4), scales=w_scales[z][:], in_=grouped[:])
+            width = H if z == 0 else P
+            for a in range(0, H, width):
+                nc.vector.quantize_mx(
+                    out=w_words[z][:, a : a + width].bitcast(FP8X4),
+                    scales=w_scales[z][:, a : a + width],
+                    in_=grouped[:, a * PACK : (a + width) * PACK],
+                )
 
         banks = {}
 
         def layer_pass(z, e):
-            if z == 0:
+            opens = e not in banks
+            if opens:
                 banks[e] = psum.tile([P, PACK, CHUNK], F32, name="bank_%d" % e, tag="bank_%d" % e)
             g, cols = e // 2, slice((e % 2) * CHUNK, (e % 2 + 1) * CHUNK)
             for t in range(PACK):
@@ -142,8 +149,8 @@ def tile_picked_haar_relu_e_kernel(
                     lhsT_scale=w_scales[z][:, m],
                     rhs=picked_words[z, g][:, cols].bitcast(FP8X4),
                     rhs_scale=picked_bytes[g][4 * z : P, cols],
-                    start=(z == 0 and t == 0),
-                    stop=(z == PASSES - 1 and t == PACK - 1),
+                    start=(opens and t == 0),
+                    stop=(not opens and t == PACK - 1),
                 )
 
         bands = {}
@@ -176,35 +183,49 @@ def tile_picked_haar_relu_e_kernel(
                     scales=scales[:, i * w : (i + 1) * w],
                     in_=both[:, i * w * PACK : (i + 1) * w * PACK],
                 )
-            acc = psum.tile([P, 2, CHUNK], F32, name="acc_%d" % c, tag="bank_%d" % (4 + c))
-            for h in range(2):
-                for band in range(2):
-                    cols = slice(band * CHUNK, (band + 1) * CHUNK)
-                    nc.tensor.matmul_mx(
-                        out=acc[:, h, :],
-                        lhsT=band_words[band][:, h * P : (h + 1) * P].bitcast(FP8X4),
-                        lhsT_scale=band_scales[:, band * N + h * P : band * N + (h + 1) * P],
-                        rhs=words[:, cols].bitcast(FP8X4),
-                        rhs_scale=scales[:, cols],
-                        start=(band == 0),
-                        stop=(band == 1),
-                    )
-            result = keep.tile([P, 2, CHUNK], F32, name="result_%d" % c)
-            nc.scalar.activation(out=result[:], in_=acc[:], func=ACT.Copy)
-            nc.sync.dma_start(out=out_view[:, :, c * CHUNK : (c + 1) * CHUNK], in_=result[:])
+            if c < 3:
+                acc = psum.tile([P, 2, CHUNK], F32, name="acc_%d" % c, tag="bank_%d" % (4 + c))
+                accs = [acc[:, 0, :], acc[:, 1, :]]
+                order = [(0, 0), (0, 1), (1, 0), (1, 1)]
+            else:
+                accs = [psum.tile([P, CHUNK], F32, name="acc_3_%d" % h, tag="bank_%d" % (7, 2)[h])[:] for h in range(2)]
+                order = [(0, 0), (1, 0), (0, 1), (1, 1)]
+            for h, band in order:
+                cols = slice(band * CHUNK, (band + 1) * CHUNK)
+                nc.tensor.matmul_mx(
+                    out=accs[h],
+                    lhsT=band_words[band][:, h * P : (h + 1) * P].bitcast(FP8X4),
+                    lhsT_scale=band_scales[:, band * N + h * P : band * N + (h + 1) * P],
+                    rhs=words[:, cols].bitcast(FP8X4),
+                    rhs_scale=scales[:, cols],
+                    start=(band == 0),
+                    stop=(band == 1),
+                )
+            cols = slice(c * CHUNK, (c + 1) * CHUNK)
+            if c < 3:
+                result = keep.tile([P, 2, CHUNK], F32, name="result_%d" % c)
+                nc.scalar.activation(out=result[:], in_=acc[:], func=ACT.Copy)
+                nc.sync.dma_start(out=out_view[:, :, cols], in_=result[:])
+            else:
+                upper = keep.tile([P, CHUNK], F32, name="result_upper")
+                lower = keep.tile([P, CHUNK], F32, name="result_lower")
+                nc.vector.tensor_copy(out=upper[:], in_=accs[0])
+                nc.sync.dma_start(out=out_view[:, 0, cols], in_=upper[:])
+                nc.scalar.activation(out=lower[:], in_=accs[1], func=ACT.Copy)
+                nc.scalar.dma_start(out=out_view[:, 1, cols], in_=lower[:])
 
         gather_bytes((2, 0), "early_bytes")
         gather_words((2, 0), "early_words")
+        gather_words((3, 1), "late_words")
         quantise_w1(0)
-        for e in (4, 0, 5, 1):
+        for e in (4, 0):
             layer_pass(0, e)
-        gather_words((3, 1), "w_raw_0")
         quantise_w1(1)
-        for e in (4, 0, 5, 1):
+        for e in (4, 0):
             layer_pass(1, e)
-        gather_bytes((3, 1), "w_bf16")
-        for e in (6, 2, 7, 3):
-            for z in range(PASSES):
+        gather_bytes((3, 1), "w_bf16_1")
+        for e in (5, 1, 6, 2, 7, 3):
+            for z in (1, 0):
                 layer_pass(z, e)
         haar(0)
         for c in range(1, 4):

@@ -23,7 +23,8 @@ CHUNK = 128
 GROUP = 256
 LIST_COL = 16
 
-X_LOADS = [[1024, 1024], [1024, 512, 256, 256]]
+X_LOADS = [[(2048, 1280)], [(2048, 1280)], [(2048, 1024)], [(1024, 0), (512, 512), (256, 0), (256, 160)]]
+CAST_PIECE = 512
 W_SCALAR = [128, 72]
 
 
@@ -36,19 +37,18 @@ def tile_picked_haar_relu_e_kernel(
         psum = ctx.enter_context(tc.psum_pool(name="psum", bufs=1))
 
         offsets = keep.tile([P, S // LIST_COL], U16, name="offsets")
-        x_bytes = keep.tile([P, T], U8, name="x_bytes", align_bytes=64)
         band_scales = keep.tile([P, 2 * N], U8, name="band_scales", align_bytes=64)
-        nc.gpsimd.memset(x_bytes[:].bitcast(I32), 0)
         nc.gpsimd.memset(band_scales[:].bitcast(I32), 0)
         x_raw = []
-        for z in range(PASSES):
+        for pair, loads in enumerate(X_LOADS):
+            z, u = divmod(pair, 2)
+            rows = xT[z * K_PASS : (z + 1) * K_PASS, :].rearrange("(p j) t -> p j t", j=PACK)
             t0 = 0
-            for width in X_LOADS[z]:
-                raw = keep.tile([P, PACK, width], F32, name="x_raw_%d_%d" % (z, t0))
-                rows = xT[z * K_PASS : (z + 1) * K_PASS, t0 : t0 + width]
-                nc.sync.dma_start(out=raw[:], in_=rows.rearrange("(p j) t -> p j t", j=PACK))
-                x_raw.append((z, t0, width, raw))
-                if z == 0 and t0 == 0:
+            for width, on_vector in loads:
+                raw = keep.tile([P, 2, width], F32, name="x_raw_%d_%d" % (pair, t0))
+                nc.sync.dma_start(out=raw[:], in_=rows[:, 2 * u : 2 * u + 2, t0 : t0 + width])
+                x_raw.append((pair, t0, width, on_vector, raw))
+                if pair == 0:
                     nc.sync.dma_start(offsets[:], offs)
                 t0 = t0 + width
         w_raw = []
@@ -73,46 +73,64 @@ def tile_picked_haar_relu_e_kernel(
                     in_=scales[0, 4 * q : 4 * q + 4, :].bitcast(I32),
                 )
 
-        x_words = [keep.tile([P, T], U32, name="x_words_%d" % z, align_bytes=64) for z in range(PASSES)]
-        picked_words = {}
-        for z, t0, width, raw in x_raw:
-            step = min(256, width // 2)
-            for a in range(0, width, step):
-                grouped = keep.tile([P, step * PACK], BF16, name="x_bf16_%d_%d" % (z, t0 + a), align_bytes=64)
-                dst = grouped[:].rearrange("p (c i j) -> p c j i", i=4, j=PACK)
-                src = raw[:, :, a : a + step].rearrange("p j (c i) -> p c j i", i=4)
-                if (a // step) % 2 == 0:
-                    nc.vector.tensor_copy(out=dst, in_=src)
-                else:
-                    nc.scalar.activation(out=dst, in_=src, func=ACT.Copy)
-                cols = slice(t0 + a, t0 + a + step)
-                nc.vector.quantize_mx(
-                    out=x_words[z][:, cols].bitcast(FP8X4),
-                    scales=x_bytes[4 * z : P, cols],
-                    in_=grouped[:],
+        windows = [keep.tile([P, 2 * T], BF16, name="window_%d" % pair, align_bytes=64) for pair in range(4)]
+
+        def cast(pair):
+            for which, t0, width, on_vector, raw in x_raw:
+                if which != pair:
+                    continue
+                for lo, hi, vector in ((0, on_vector, True), (on_vector, width, False)):
+                    if hi == lo:
+                        continue
+                    dst = windows[pair][:, 2 * (t0 + lo) : 2 * (t0 + hi)].rearrange("p (c i e) -> p c e i", i=4, e=2)
+                    src = raw[:, :, lo:hi].rearrange("p e (c i) -> p c e i", i=4)
+                    if vector:
+                        nc.vector.tensor_copy(out=dst, in_=src)
+                    else:
+                        nc.scalar.activation(out=dst, in_=src, func=ACT.Copy)
+
+        picked = {}
+        for z in range(PASSES):
+            for g in range(S // GROUP):
+                picked[z, g] = keep.tile([P, 2, GROUP], U32, name="picked_%d_%d" % (z, g), align_bytes=64)
+
+        def gather(pair, g):
+            z, u = divmod(pair, 2)
+            piece = offsets[:, g * GROUP // LIST_COL : (g + 1) * GROUP // LIST_COL]
+            nc.vector.tensor_copy(out=picked[z, g][:, u, :], in_=windows[pair][:].bitcast(U32).indirect(piece))
+
+        woven, x_words, x_scales = {}, {}, {}
+
+        def weave(z, g, tag):
+            woven[z, g] = keep.tile([P, GROUP * PACK], BF16, name="woven_%d_%d" % (z, g), tag=tag, align_bytes=64)
+            src = picked[z, g][:].rearrange("p u n -> p n u")
+            if z == 0:
+                nc.scalar.copy(out=woven[z, g][:].bitcast(U32).rearrange("p (n u) -> p n u", u=2), in_=src)
+            else:
+                nc.vector.tensor_copy(
+                    out=woven[z, g][:].bitcast(I32).rearrange("p (n u) -> p n u", u=2),
+                    in_=picked[z, g][:].bitcast(I32).rearrange("p u n -> p n u"),
                 )
-            if z == 0 and t0 + width == T:
-                first = keep.tile([P, S], U32, name="picked_words_0", align_bytes=64)
-                nc.vector.tensor_copy(out=first[:], in_=x_words[0][:].indirect(offsets[:]))
-                for g in range(S // GROUP):
-                    picked_words[0, g] = first[:, g * GROUP : (g + 1) * GROUP]
 
-        picked_bytes = {}
+        def quantise_x(z, g):
+            x_words[z, g] = keep.tile([P, GROUP], U32, name="x_words_%d_%d" % (z, g), align_bytes=64)
+            x_scales[z, g] = keep.tile([P, GROUP], U8, name="x_scales_%d_%d" % (z, g), align_bytes=64)
+            nc.vector.quantize_mx(out=x_words[z, g][:].bitcast(FP8X4), scales=x_scales[z, g][:], in_=woven[z, g][:])
 
-        def piece(g):
-            return offsets[:, g * GROUP // LIST_COL : (g + 1) * GROUP // LIST_COL]
-
-        def gather_bytes(groups, tag):
-            by = keep.tile([P, 2 * GROUP], U8, name="picked_bytes_%d" % groups[0], tag=tag, align_bytes=64)
-            for i, g in enumerate(groups):
-                picked_bytes[g] = by[:, i * GROUP : (i + 1) * GROUP]
-                nc.vector.tensor_copy(out=picked_bytes[g], in_=x_bytes[:].indirect(piece(g)))
-
-        def gather_words(groups, tag):
-            wo = keep.tile([P, 2 * GROUP], U32, name="picked_words_1_%d" % groups[0], tag=tag, align_bytes=64)
-            for i, g in enumerate(groups):
-                picked_words[1, g] = wo[:, i * GROUP : (i + 1) * GROUP]
-                nc.vector.tensor_copy(out=picked_words[1, g], in_=x_words[1][:].indirect(piece(g)))
+        ORDER = (2, 0, 3, 1)
+        cast(0)
+        for g in ORDER:
+            gather(0, g)
+        cast(1)
+        for g in ORDER:
+            gather(1, g)
+        for g in ORDER:
+            weave(0, g, "woven_0_%d" % g)
+            quantise_x(0, g)
+        cast(2)
+        for g in ORDER:
+            gather(2, g)
+        cast(3)
 
         w_words, w_scales = {}, {}
 
@@ -147,8 +165,8 @@ def tile_picked_haar_relu_e_kernel(
                     out=banks[e][:, t, :],
                     lhsT=w_words[z][:, m].bitcast(FP8X4),
                     lhsT_scale=w_scales[z][:, m],
-                    rhs=picked_words[z, g][:, cols].bitcast(FP8X4),
-                    rhs_scale=picked_bytes[g][4 * z : P, cols],
+                    rhs=x_words[z, g][:, cols].bitcast(FP8X4),
+                    rhs_scale=x_scales[z, g][:, cols],
                     start=(opens and t == 0),
                     stop=(not opens and t == PACK - 1),
                 )
@@ -214,16 +232,22 @@ def tile_picked_haar_relu_e_kernel(
                 nc.scalar.activation(out=lower[:], in_=accs[1], func=ACT.Copy)
                 nc.scalar.dma_start(out=out_view[:, 1, cols], in_=lower[:])
 
-        gather_bytes((2, 0), "early_bytes")
-        gather_words((2, 0), "early_words")
-        gather_words((3, 1), "late_words")
+        for g in ORDER:
+            gather(3, g)
+        for g in (2, 0):
+            weave(1, g, "woven_1_%d" % g)
+        for g in (2, 0):
+            quantise_x(1, g)
         quantise_w1(0)
         for e in (4, 0):
             layer_pass(0, e)
         quantise_w1(1)
         for e in (4, 0):
             layer_pass(1, e)
-        gather_bytes((3, 1), "w_bf16_1")
+        weave(1, 3, "w_bf16_1")
+        weave(1, 1, "w_raw_1")
+        for g in (3, 1):
+            quantise_x(1, g)
         for e in (5, 1, 6, 2, 7, 3):
             for z in (1, 0):
                 layer_pass(z, e)

@@ -23,9 +23,13 @@ CHUNK = 128
 GROUP = 256
 LIST_COL = 16
 
-X_LOADS = [[(2048, 1280)], [(2048, 1280)], [(2048, 1024)], [(1024, 0), (512, 512), (256, 0), (256, 160)]]
-CAST_PIECE = 512
-W_SCALAR = [128, 72]
+X_LOADS = [
+    [(2048, 1248)],
+    [(1024, 0), (1024, 624)],
+    [(1024, 0), (1024, 624)],
+    [(512, 0), (512, 0), (512, 0), (256, 0), (256, 256)],
+]
+W_SCALAR = [0, 70]
 
 
 def tile_picked_haar_relu_e_kernel(
@@ -39,16 +43,17 @@ def tile_picked_haar_relu_e_kernel(
         offsets = keep.tile([P, S // LIST_COL], U16, name="offsets")
         band_scales = keep.tile([P, 2 * N], U8, name="band_scales", align_bytes=64)
         nc.gpsimd.memset(band_scales[:].bitcast(I32), 0)
-        x_raw = []
+        x_raw = {}
         for pair, loads in enumerate(X_LOADS):
             z, u = divmod(pair, 2)
             rows = xT[z * K_PASS : (z + 1) * K_PASS, :].rearrange("(p j) t -> p j t", j=PACK)
             t0 = 0
-            for width, on_vector in loads:
-                raw = keep.tile([P, 2, width], F32, name="x_raw_%d_%d" % (pair, t0))
+            for i, (width, on_vector) in enumerate(loads):
+                name = "x_raw_%d_%d" % (pair, i)
+                raw = keep.tile([P, 2, width], F32, name=name, tag=name, align_bytes=64)
                 nc.sync.dma_start(out=raw[:], in_=rows[:, 2 * u : 2 * u + 2, t0 : t0 + width])
-                x_raw.append((pair, t0, width, on_vector, raw))
-                if pair == 0:
+                x_raw[pair, i] = (t0, width, on_vector, raw)
+                if pair == 0 and i == 0:
                     nc.sync.dma_start(offsets[:], offs)
                 t0 = t0 + width
         w_raw = []
@@ -75,73 +80,92 @@ def tile_picked_haar_relu_e_kernel(
 
         windows = [keep.tile([P, 2 * T], BF16, name="window_%d" % pair, align_bytes=64) for pair in range(4)]
 
-        def cast(pair):
-            for which, t0, width, on_vector, raw in x_raw:
-                if which != pair:
+        def cast(pair, i):
+            t0, width, on_vector, raw = x_raw[pair, i]
+            for lo, hi, vector in ((0, on_vector, True), (on_vector, width, False)):
+                if hi == lo:
                     continue
-                for lo, hi, vector in ((0, on_vector, True), (on_vector, width, False)):
-                    if hi == lo:
-                        continue
-                    dst = windows[pair][:, 2 * (t0 + lo) : 2 * (t0 + hi)].rearrange("p (c i e) -> p c e i", i=4, e=2)
-                    src = raw[:, :, lo:hi].rearrange("p e (c i) -> p c e i", i=4)
-                    if vector:
-                        nc.vector.tensor_copy(out=dst, in_=src)
-                    else:
-                        nc.scalar.activation(out=dst, in_=src, func=ACT.Copy)
+                dst = windows[pair][:, 2 * (t0 + lo) : 2 * (t0 + hi)].rearrange("p (c i e) -> p c e i", i=4, e=2)
+                src = raw[:, :, lo:hi].rearrange("p e (c i) -> p c e i", i=4)
+                if vector:
+                    nc.vector.tensor_copy(out=dst, in_=src)
+                else:
+                    nc.scalar.activation(out=dst, in_=src, func=ACT.Copy)
 
+        ORDER = (2, 0, 3, 1)
         picked = {}
-        for z in range(PASSES):
-            for g in range(S // GROUP):
-                picked[z, g] = keep.tile([P, 2, GROUP], U32, name="picked_%d_%d" % (z, g), align_bytes=64)
+        for key in [(0, g) for g in ORDER] + [(1, g) for g in ORDER[:2]]:
+            name = "picked_%d_%d" % key
+            picked[key] = keep.tile([P, 2, GROUP], U32, name=name, tag=name, align_bytes=64)[:]
+        shared = keep.tile([P, 2 * GROUP + H * PACK // 2], U32, name="shared", align_bytes=64)
+        for i, g in enumerate(ORDER[2:]):
+            picked[1, g] = shared[:, : 4 * GROUP].rearrange("p (u g n) -> p g u n", u=2, g=2)[:, i]
 
         def gather(pair, g):
             z, u = divmod(pair, 2)
             piece = offsets[:, g * GROUP // LIST_COL : (g + 1) * GROUP // LIST_COL]
             nc.vector.tensor_copy(out=picked[z, g][:, u, :], in_=windows[pair][:].bitcast(U32).indirect(piece))
 
-        woven, x_words, x_scales = {}, {}, {}
+        x_words, x_scales = {}, {}
 
-        def weave(z, g, tag):
-            woven[z, g] = keep.tile([P, GROUP * PACK], BF16, name="woven_%d_%d" % (z, g), tag=tag, align_bytes=64)
-            src = picked[z, g][:].rearrange("p u n -> p n u")
-            if z == 0:
-                nc.scalar.copy(out=woven[z, g][:].bitcast(U32).rearrange("p (n u) -> p n u", u=2), in_=src)
-            else:
-                nc.vector.tensor_copy(
-                    out=woven[z, g][:].bitcast(I32).rearrange("p (n u) -> p n u", u=2),
-                    in_=picked[z, g][:].bitcast(I32).rearrange("p u n -> p n u"),
-                )
+        def weave(sets, tag, on_vector=False):
+            woven = keep.tile([P, len(sets) * GROUP * PACK], BF16, name="woven_%d_%d" % sets[0], tag=tag, align_bytes=64)
+            for i, key in enumerate(sets):
+                dst = woven[:, i * GROUP * PACK : (i + 1) * GROUP * PACK]
+                if on_vector:
+                    nc.vector.tensor_copy(
+                        out=dst.bitcast(I32).rearrange("p (n u) -> p n u", u=2),
+                        in_=picked[key].bitcast(I32).rearrange("p u n -> p n u"),
+                    )
+                else:
+                    nc.scalar.copy(
+                        out=dst.bitcast(U32).rearrange("p (n u) -> p n u", u=2), in_=picked[key].rearrange("p u n -> p n u")
+                    )
+            return woven
 
-        def quantise_x(z, g):
-            x_words[z, g] = keep.tile([P, GROUP], U32, name="x_words_%d_%d" % (z, g), align_bytes=64)
-            x_scales[z, g] = keep.tile([P, GROUP], U8, name="x_scales_%d_%d" % (z, g), align_bytes=64)
-            nc.vector.quantize_mx(out=x_words[z, g][:].bitcast(FP8X4), scales=x_scales[z, g][:], in_=woven[z, g][:])
+        def quantise_x(sets, woven, tag):
+            count = len(sets) * GROUP
+            words = keep.tile([P, count], U32, name="x_words_%d_%d" % sets[0], tag=tag, align_bytes=64)
+            scales = keep.tile([P, count], U8, name="x_scales_%d_%d" % sets[0], align_bytes=64)
+            nc.vector.quantize_mx(out=words[:].bitcast(FP8X4), scales=scales[:], in_=woven[:])
+            for i, key in enumerate(sets):
+                x_words[key] = words[:, i * GROUP : (i + 1) * GROUP]
+                x_scales[key] = scales[:, i * GROUP : (i + 1) * GROUP]
 
-        ORDER = (2, 0, 3, 1)
-        cast(0)
+        early = [[(z, g) for g in ORDER[:2]] for z in range(PASSES)]
+        late = [[(z, g) for g in ORDER[2:]] for z in range(PASSES)]
+        cast(0, 0)
         for g in ORDER:
             gather(0, g)
-        cast(1)
+        cast(1, 0)
+        cast(1, 1)
         for g in ORDER:
             gather(1, g)
-        for g in ORDER:
-            weave(0, g, "woven_0_%d" % g)
-            quantise_x(0, g)
-        cast(2)
+        woven_early = weave(early[0], "woven_early_0", on_vector=True)
+        cast(2, 0)
+        cast(2, 1)
         for g in ORDER:
             gather(2, g)
-        cast(3)
+        quantise_x(early[0], woven_early, "x_raw_2_1")
+        for i in range(len(X_LOADS[3])):
+            cast(3, i)
 
         w_words, w_scales = {}, {}
 
-        def quantise_w1(z):
-            grouped = keep.tile([P, H * PACK], BF16, name="w_bf16_%d" % z, tag="w_bf16_%d" % z, align_bytes=64)
-            dst = grouped[:].rearrange("p (t m j) -> p m j t", t=PACK, j=PACK)
+        def cast_w1(z):
+            if z == 0:
+                grouped = keep.tile([P, H * PACK], BF16, name="w_bf16_0", align_bytes=64)[:]
+            else:
+                grouped = shared[:, 2 * GROUP :].bitcast(BF16)
+            dst = grouped.rearrange("p (t m j) -> p m j t", t=PACK, j=PACK)
             src = w_raw[z][:].rearrange("p j (m t) -> p m j t", t=PACK)
             cut = W_SCALAR[z]
-            nc.scalar.activation(out=dst[:, :cut], in_=src[:, :cut], func=ACT.Copy, scale=0.5)
-            if cut < P:
-                nc.vector.tensor_scalar(out=dst[:, cut:], in0=src[:, cut:], scalar1=0.5, scalar2=None, op0=ALU.mult)
+            if cut > 0:
+                nc.scalar.activation(out=dst[:, :cut], in_=src[:, :cut], func=ACT.Copy, scale=0.5)
+            nc.vector.tensor_scalar(out=dst[:, cut:], in0=src[:, cut:], scalar1=0.5, scalar2=None, op0=ALU.mult)
+            return grouped
+
+        def quantise_w1(z, grouped):
             w_words[z] = keep.tile([P, H], U32, name="w_words_%d" % z, align_bytes=64)
             w_scales[z] = keep.tile([P, H], U8, name="w_scales_%d" % z, align_bytes=64)
             width = H if z == 0 else P
@@ -154,8 +178,7 @@ def tile_picked_haar_relu_e_kernel(
 
         banks = {}
 
-        def layer_pass(z, e):
-            opens = e not in banks
+        def layer_pass(z, e, opens):
             if opens:
                 banks[e] = psum.tile([P, PACK, CHUNK], F32, name="bank_%d" % e, tag="bank_%d" % e)
             g, cols = e // 2, slice((e % 2) * CHUNK, (e % 2 + 1) * CHUNK)
@@ -171,21 +194,23 @@ def tile_picked_haar_relu_e_kernel(
                     stop=(not opens and t == PACK - 1),
                 )
 
-        bands = {}
+        bands, seconds = {}, {}
 
-        def haar(c):
-            second = keep.tile([P, CHUNK, PACK], F32, name="second_%d" % c)
-            nc.scalar.activation(out=second[:], in_=banks[4 + c][:].rearrange("p t n -> p n t"), func=ACT.Relu)
-            bands[c] = keep.tile([P, 2, CHUNK, PACK], BF16, name="bands_%d" % c, align_bytes=64)
-            for band, op in enumerate((ALU.add, ALU.subtract)):
-                nc.vector.scalar_tensor_tensor(
-                    out=bands[c][:, band],
-                    in0=banks[c][:].rearrange("p t n -> p n t"),
-                    scalar=0.0,
-                    in1=second[:],
-                    op0=ALU.max,
-                    op1=op,
-                )
+        def relu_second(c):
+            seconds[c] = keep.tile([P, CHUNK, PACK], F32, name="second_%d" % c)
+            nc.scalar.activation(out=seconds[c][:], in_=banks[4 + c][:].rearrange("p t n -> p n t"), func=ACT.Relu)
+
+        def haar(c, band):
+            if band == 0:
+                bands[c] = keep.tile([P, 2, CHUNK, PACK], BF16, name="bands_%d" % c, align_bytes=64)
+            nc.vector.scalar_tensor_tensor(
+                out=bands[c][:, band],
+                in0=banks[c][:].rearrange("p t n -> p n t"),
+                scalar=0.0,
+                in1=seconds[c][:],
+                op0=ALU.max,
+                op1=(ALU.add, ALU.subtract)[band],
+            )
 
         out_view = out.rearrange("(h m) v -> m h v", m=P)
 
@@ -232,27 +257,36 @@ def tile_picked_haar_relu_e_kernel(
                 nc.scalar.activation(out=lower[:], in_=accs[1], func=ACT.Copy)
                 nc.scalar.dma_start(out=out_view[:, 1, cols], in_=lower[:])
 
-        for g in ORDER:
+        for g in ORDER[:2]:
             gather(3, g)
-        for g in (2, 0):
-            weave(1, g, "woven_1_%d" % g)
-        for g in (2, 0):
-            quantise_x(1, g)
-        quantise_w1(0)
+        woven_early = weave(early[1], "woven_early_1")
+        woven_late = weave(late[0], "picked_1_0")
+        grouped = cast_w1(0)
+        quantise_x(early[1], woven_early, "w_raw_0")
+        quantise_w1(0, grouped)
+        quantise_w1(1, cast_w1(1))
+        for g in ORDER[2:]:
+            gather(3, g)
+        quantise_x(late[0], woven_late, "w_raw_1")
+
         for e in (4, 0):
-            layer_pass(0, e)
-        quantise_w1(1)
-        for e in (4, 0):
-            layer_pass(1, e)
-        weave(1, 3, "w_bf16_1")
-        weave(1, 1, "w_raw_1")
-        for g in (3, 1):
-            quantise_x(1, g)
-        for e in (5, 1, 6, 2, 7, 3):
+            for z in (0, 1):
+                layer_pass(z, e, z == 0)
+        for e in (5, 1):
             for z in (1, 0):
-                layer_pass(z, e)
-        haar(0)
+                layer_pass(z, e, z == 1)
+        relu_second(0)
+        haar(0, 0)
+        haar(0, 1)
+        relu_second(1)
+        quantise_x(late[1], weave(late[1], "woven_late_1"), "x_words_late_1")
+        for e in (6, 2, 7, 3):
+            for z in (0, 1):
+                layer_pass(z, e, z == 0)
         for c in range(1, 4):
-            haar(c)
+            if c > 1:
+                relu_second(c)
+            haar(c, 0)
             finish(c - 1)
+            haar(c, 1)
         finish(3)

@@ -24,12 +24,12 @@ GROUP = 256
 LIST_COL = 16
 
 X_LOADS = [
-    [(2048, 1248)],
-    [(1024, 0), (1024, 624)],
-    [(1024, 0), (1024, 624)],
-    [(512, 0), (512, 0), (512, 0), (256, 0), (256, 256)],
+    [(2048, 1360)],
+    [(2048, 1360)],
+    [(2048, 1408)],
+    [(1024, 0), (1024, 672)],
 ]
-W_SCALAR = [0, 70]
+W_SCALAR = [128, 74]
 
 
 def tile_picked_haar_relu_e_kernel(
@@ -94,12 +94,9 @@ def tile_picked_haar_relu_e_kernel(
 
         ORDER = (2, 0, 3, 1)
         picked = {}
-        for key in [(0, g) for g in ORDER] + [(1, g) for g in ORDER[:2]]:
-            name = "picked_%d_%d" % key
-            picked[key] = keep.tile([P, 2, GROUP], U32, name=name, tag=name, align_bytes=64)[:]
-        shared = keep.tile([P, 2 * GROUP + H * PACK // 2], U32, name="shared", align_bytes=64)
-        for i, g in enumerate(ORDER[2:]):
-            picked[1, g] = shared[:, : 4 * GROUP].rearrange("p (u g n) -> p g u n", u=2, g=2)[:, i]
+        for z in range(PASSES):
+            for g in ORDER:
+                picked[z, g] = keep.tile([P, 2, GROUP], U32, name="picked_%d_%d" % (z, g), align_bytes=64)[:]
 
         def gather(pair, g):
             z, u = divmod(pair, 2)
@@ -134,41 +131,35 @@ def tile_picked_haar_relu_e_kernel(
 
         early = [[(z, g) for g in ORDER[:2]] for z in range(PASSES)]
         late = [[(z, g) for g in ORDER[2:]] for z in range(PASSES)]
-        cast(0, 0)
-        for g in ORDER:
-            gather(0, g)
-        cast(1, 0)
-        cast(1, 1)
-        for g in ORDER:
-            gather(1, g)
-        woven_early = weave(early[0], "woven_early_0", on_vector=True)
+        for pair in range(2):
+            cast(pair, 0)
+            for g in ORDER:
+                gather(pair, g)
+        quantise_x(early[0], weave(early[0], "woven_early_0"), "x_words_early_0")
+        woven_late = weave(late[0], "woven_late_0")
         cast(2, 0)
-        cast(2, 1)
         for g in ORDER:
             gather(2, g)
-        quantise_x(early[0], woven_early, "x_raw_2_1")
         for i in range(len(X_LOADS[3])):
             cast(3, i)
 
         w_words, w_scales = {}, {}
 
         def cast_w1(z):
-            if z == 0:
-                grouped = keep.tile([P, H * PACK], BF16, name="w_bf16_0", align_bytes=64)[:]
-            else:
-                grouped = shared[:, 2 * GROUP :].bitcast(BF16)
+            name = "w_bf16_%d" % z
+            grouped = keep.tile([P, H * PACK], BF16, name=name, tag=name, align_bytes=64)[:]
             dst = grouped.rearrange("p (t m j) -> p m j t", t=PACK, j=PACK)
             src = w_raw[z][:].rearrange("p j (m t) -> p m j t", t=PACK)
             cut = W_SCALAR[z]
-            if cut > 0:
-                nc.scalar.activation(out=dst[:, :cut], in_=src[:, :cut], func=ACT.Copy, scale=0.5)
-            nc.vector.tensor_scalar(out=dst[:, cut:], in0=src[:, cut:], scalar1=0.5, scalar2=None, op0=ALU.mult)
+            nc.scalar.activation(out=dst[:, :cut], in_=src[:, :cut], func=ACT.Copy, scale=0.5)
+            if cut < P:
+                nc.vector.tensor_scalar(out=dst[:, cut:], in0=src[:, cut:], scalar1=0.5, scalar2=None, op0=ALU.mult)
             return grouped
 
         def quantise_w1(z, grouped):
             w_words[z] = keep.tile([P, H], U32, name="w_words_%d" % z, align_bytes=64)
             w_scales[z] = keep.tile([P, H], U8, name="w_scales_%d" % z, align_bytes=64)
-            width = H if z == 0 else P
+            width = P
             for a in range(0, H, width):
                 nc.vector.quantize_mx(
                     out=w_words[z][:, a : a + width].bitcast(FP8X4),
@@ -257,17 +248,13 @@ def tile_picked_haar_relu_e_kernel(
                 nc.scalar.activation(out=lower[:], in_=accs[1], func=ACT.Copy)
                 nc.scalar.dma_start(out=out_view[:, 1, cols], in_=lower[:])
 
-        for g in ORDER[:2]:
+        for g in ORDER:
             gather(3, g)
-        woven_early = weave(early[1], "woven_early_1")
-        woven_late = weave(late[0], "picked_1_0")
-        grouped = cast_w1(0)
-        quantise_x(early[1], woven_early, "w_raw_0")
-        quantise_w1(0, grouped)
-        quantise_w1(1, cast_w1(1))
-        for g in ORDER[2:]:
-            gather(3, g)
-        quantise_x(late[0], woven_late, "w_raw_1")
+        quantise_x(early[1], weave(early[1], "woven_early_1", on_vector=True), "x_words_early_1")
+        for z in range(PASSES):
+            quantise_w1(z, cast_w1(z))
+        quantise_x(late[0], woven_late, "w_bf16_1")
+        quantise_x(late[1], weave(late[1], "w_raw_1"), "x_words_late_1")
 
         for e in (4, 0):
             for z in (0, 1):
@@ -275,14 +262,13 @@ def tile_picked_haar_relu_e_kernel(
         for e in (5, 1):
             for z in (1, 0):
                 layer_pass(z, e, z == 1)
+        for e in (6, 2, 7, 3):
+            for z in (0, 1):
+                layer_pass(z, e, z == 0)
         relu_second(0)
         haar(0, 0)
         haar(0, 1)
         relu_second(1)
-        quantise_x(late[1], weave(late[1], "woven_late_1"), "x_words_late_1")
-        for e in (6, 2, 7, 3):
-            for z in (0, 1):
-                layer_pass(z, e, z == 0)
         for c in range(1, 4):
             if c > 1:
                 relu_second(c)

@@ -26,8 +26,8 @@ LIST_COL = 16
 X_LOADS = [
     [(2048, 1360)],
     [(2048, 1360)],
-    [(2048, 1408)],
-    [(1024, 0), (1024, 672)],
+    [(2048, 1152)],
+    [(1024, 0), (1024, 576)],
 ]
 W_SCALAR = [128, 74]
 
@@ -94,14 +94,14 @@ def tile_picked_haar_relu_e_kernel(
 
         ORDER = (2, 0, 3, 1)
         picked = {}
-        for z in range(PASSES):
-            for g in ORDER:
-                picked[z, g] = keep.tile([P, 2, GROUP], U32, name="picked_%d_%d" % (z, g), align_bytes=64)[:]
+        picked_last = keep.tile([P, 2, S], U32, name="picked_last", align_bytes=64)
+        for g in ORDER:
+            picked[0, g] = keep.tile([P, 2, GROUP], U32, name="picked_0_%d" % g, align_bytes=64)[:]
+            picked[1, g] = picked_last[:, :, g * GROUP : (g + 1) * GROUP]
 
-        def gather(pair, g):
-            z, u = divmod(pair, 2)
-            piece = offsets[:, g * GROUP // LIST_COL : (g + 1) * GROUP // LIST_COL]
-            nc.vector.tensor_copy(out=picked[z, g][:, u, :], in_=windows[pair][:].bitcast(U32).indirect(piece))
+        def gather(pair, dst, first, count):
+            piece = offsets[:, first // LIST_COL : (first + count) // LIST_COL]
+            nc.vector.tensor_copy(out=dst, in_=windows[pair][:].bitcast(U32).indirect(piece))
 
         x_words, x_scales = {}, {}
 
@@ -129,19 +129,18 @@ def tile_picked_haar_relu_e_kernel(
                 x_words[key] = words[:, i * GROUP : (i + 1) * GROUP]
                 x_scales[key] = scales[:, i * GROUP : (i + 1) * GROUP]
 
-        early = [[(z, g) for g in ORDER[:2]] for z in range(PASSES)]
+        early = [[(0, 2), (0, 0)], [(1, 0), (1, 2)]]
         late = [[(z, g) for g in ORDER[2:]] for z in range(PASSES)]
         for pair in range(2):
             cast(pair, 0)
             for g in ORDER:
-                gather(pair, g)
+                gather(pair, picked[0, g][:, pair, :], g * GROUP, GROUP)
         quantise_x(early[0], weave(early[0], "woven_early_0"), "x_words_early_0")
-        woven_late = weave(late[0], "woven_late_0")
         cast(2, 0)
-        for g in ORDER:
-            gather(2, g)
+        gather(2, picked_last[:, 0, :], 0, S)
         for i in range(len(X_LOADS[3])):
             cast(3, i)
+        woven_late = weave(late[0], "x_raw_3_1")
 
         w_words, w_scales = {}, {}
 
@@ -248,9 +247,11 @@ def tile_picked_haar_relu_e_kernel(
                 nc.scalar.activation(out=lower[:], in_=accs[1], func=ACT.Copy)
                 nc.scalar.dma_start(out=out_view[:, 1, cols], in_=lower[:])
 
-        for g in ORDER:
-            gather(3, g)
-        quantise_x(early[1], weave(early[1], "woven_early_1", on_vector=True), "x_words_early_1")
+        for first in (0, V):
+            gather(3, picked_last[:, 1, first : first + V], first, V)
+        woven_early = [weave([key], "woven_early_1_%d" % key[1], on_vector=True) for key in early[1]]
+        for key, woven in zip(early[1], woven_early):
+            quantise_x([key], woven, "x_words_early_1_%d" % key[1])
         for z in range(PASSES):
             quantise_w1(z, cast_w1(z))
         quantise_x(late[0], woven_late, "w_bf16_1")

@@ -29,7 +29,7 @@ X_LOADS = [
     [(2048, 1152)],
     [(1024, 0), (1024, 576)],
 ]
-W_SCALAR = [128, 74]
+W_SCALAR = [128, 78]
 
 
 def tile_picked_haar_relu_e_kernel(
@@ -172,7 +172,10 @@ def tile_picked_haar_relu_e_kernel(
             if opens:
                 banks[e] = psum.tile([P, PACK, CHUNK], F32, name="bank_%d" % e, tag="bank_%d" % e)
             g, cols = e // 2, slice((e % 2) * CHUNK, (e % 2 + 1) * CHUNK)
-            for t in range(PACK):
+            tiles = list(range(PACK))
+            if z == 1 and e != 4:
+                tiles = tiles[::-1]
+            for t in tiles:
                 m = slice(t * P, (t + 1) * P)
                 nc.tensor.matmul_mx(
                     out=banks[e][:, t, :],
@@ -180,27 +183,33 @@ def tile_picked_haar_relu_e_kernel(
                     lhsT_scale=w_scales[z][:, m],
                     rhs=x_words[z, g][:, cols].bitcast(FP8X4),
                     rhs_scale=x_scales[z, g][:, cols],
-                    start=(opens and t == 0),
-                    stop=(not opens and t == PACK - 1),
+                    start=(opens and t == tiles[0]),
+                    stop=(not opens and t == tiles[-1]),
                 )
 
         bands, seconds = {}, {}
 
-        def relu_second(c):
+        def relu_second(c, parts=1):
             seconds[c] = keep.tile([P, CHUNK, PACK], F32, name="second_%d" % c)
-            nc.scalar.activation(out=seconds[c][:], in_=banks[4 + c][:].rearrange("p t n -> p n t"), func=ACT.Relu)
+            src = banks[4 + c][:].rearrange("p t n -> p n t")
+            for lo in range(0, CHUNK, CHUNK // parts):
+                cols = slice(lo, lo + CHUNK // parts)
+                nc.scalar.activation(out=seconds[c][:, cols], in_=src[:, cols], func=ACT.Relu)
 
-        def haar(c, band):
+        def haar(c, band, parts=1):
             if band == 0:
                 bands[c] = keep.tile([P, 2, CHUNK, PACK], BF16, name="bands_%d" % c, align_bytes=64)
-            nc.vector.scalar_tensor_tensor(
-                out=bands[c][:, band],
-                in0=banks[c][:].rearrange("p t n -> p n t"),
-                scalar=0.0,
-                in1=seconds[c][:],
-                op0=ALU.max,
-                op1=(ALU.add, ALU.subtract)[band],
-            )
+            src = banks[c][:].rearrange("p t n -> p n t")
+            for lo in range(0, CHUNK, CHUNK // parts):
+                cols = slice(lo, lo + CHUNK // parts)
+                nc.vector.scalar_tensor_tensor(
+                    out=bands[c][:, band, cols],
+                    in0=src[:, cols],
+                    scalar=0.0,
+                    in1=seconds[c][:, cols],
+                    op0=ALU.max,
+                    op1=(ALU.add, ALU.subtract)[band],
+                )
 
         out_view = out.rearrange("(h m) v -> m h v", m=P)
 
@@ -255,7 +264,7 @@ def tile_picked_haar_relu_e_kernel(
         for z in range(PASSES):
             quantise_w1(z, cast_w1(z))
         quantise_x(late[0], woven_late, "w_bf16_1")
-        quantise_x(late[1], weave(late[1], "w_raw_1"), "x_words_late_1")
+        quantise_x(late[1], weave(late[1], "w_bf16_0"), "x_words_late_1")
 
         for e in (4, 0):
             for z in (0, 1):
@@ -266,8 +275,8 @@ def tile_picked_haar_relu_e_kernel(
         for e in (6, 2, 7, 3):
             for z in (0, 1):
                 layer_pass(z, e, z == 0)
-        relu_second(0)
-        haar(0, 0)
+        relu_second(0, parts=2)
+        haar(0, 0, parts=2)
         haar(0, 1)
         relu_second(1)
         for c in range(1, 4):

@@ -26,10 +26,10 @@ LIST_COL = 16
 X_LOADS = [
     [(2048, 1360)],
     [(2048, 1360)],
-    [(2048, 1152)],
-    [(1024, 0), (1024, 576)],
+    [(2048, 1216)],
+    [(1024, 0), (1024, 640)],
 ]
-W_SCALAR = [128, 78]
+W_LAST_SCALAR = 28
 
 
 def tile_picked_haar_relu_e_kernel(
@@ -144,27 +144,25 @@ def tile_picked_haar_relu_e_kernel(
 
         w_words, w_scales = {}, {}
 
-        def cast_w1(z):
-            name = "w_bf16_%d" % z
-            grouped = keep.tile([P, H * PACK], BF16, name=name, tag=name, align_bytes=64)[:]
-            dst = grouped.rearrange("p (t m j) -> p m j t", t=PACK, j=PACK)
-            src = w_raw[z][:].rearrange("p j (m t) -> p m j t", t=PACK)
-            cut = W_SCALAR[z]
-            nc.scalar.activation(out=dst[:, :cut], in_=src[:, :cut], func=ACT.Copy, scale=0.5)
-            if cut < P:
-                nc.vector.tensor_scalar(out=dst[:, cut:], in0=src[:, cut:], scalar1=0.5, scalar2=None, op0=ALU.mult)
-            return grouped
+        def round_w1(z, tiles, parts):
+            name = "w_bf16_%d_%d" % (z, tiles.start)
+            count = tiles.stop - tiles.start
+            grouped = keep.tile([P, count * P * PACK], BF16, name=name, tag=name, align_bytes=64)
+            dst = grouped[:].rearrange("p (t m j) -> p m j t", m=P, j=PACK)
+            src = w_raw[z][:].rearrange("p j (m t) -> p m j t", t=PACK)[:, :, :, tiles]
+            for cols, on_vector in parts:
+                if on_vector:
+                    nc.vector.tensor_scalar(out=dst[:, cols], in0=src[:, cols], scalar1=0.5, scalar2=None, op0=ALU.mult)
+                else:
+                    nc.scalar.activation(out=dst[:, cols], in_=src[:, cols], func=ACT.Copy, scale=0.5)
+            return [grouped[:, i * P * PACK : (i + 1) * P * PACK] for i in range(count)]
 
-        def quantise_w1(z, grouped):
+        def quantise_w1(z, rounded):
             w_words[z] = keep.tile([P, H], U32, name="w_words_%d" % z, align_bytes=64)
             w_scales[z] = keep.tile([P, H], U8, name="w_scales_%d" % z, align_bytes=64)
-            width = P
-            for a in range(0, H, width):
-                nc.vector.quantize_mx(
-                    out=w_words[z][:, a : a + width].bitcast(FP8X4),
-                    scales=w_scales[z][:, a : a + width],
-                    in_=grouped[:, a * PACK : (a + width) * PACK],
-                )
+            for t in range(PACK):
+                m = slice(t * P, (t + 1) * P)
+                nc.vector.quantize_mx(out=w_words[z][:, m].bitcast(FP8X4), scales=w_scales[z][:, m], in_=rounded[t])
 
         banks = {}
 
@@ -261,17 +259,18 @@ def tile_picked_haar_relu_e_kernel(
         woven_early = [weave([key], "woven_early_1_%d" % key[1], on_vector=True) for key in early[1]]
         for key, woven in zip(early[1], woven_early):
             quantise_x([key], woven, "x_words_early_1_%d" % key[1])
-        for z in range(PASSES):
-            quantise_w1(z, cast_w1(z))
-        quantise_x(late[0], woven_late, "w_bf16_1")
-        quantise_x(late[1], weave(late[1], "w_bf16_0"), "x_words_late_1")
+        quantise_w1(0, round_w1(0, slice(0, PACK), [(slice(0, P), False)]))
+        rounded = round_w1(1, slice(0, 2), [(slice(0, P), False)])
+        rounded = rounded + round_w1(1, slice(2, PACK), [(slice(0, W_LAST_SCALAR), False), (slice(W_LAST_SCALAR, P), True)])
+        quantise_w1(1, rounded)
+        quantise_x(late[0], woven_late, "w_bf16_1_2")
+        quantise_x(late[1], weave(late[1], "w_bf16_0_0"), "x_words_late_1")
 
-        for e in (4, 0):
+        for e in (4, 0, 5):
             for z in (0, 1):
                 layer_pass(z, e, z == 0)
-        for e in (5, 1):
-            for z in (1, 0):
-                layer_pass(z, e, z == 1)
+        for z in (1, 0):
+            layer_pass(z, 1, z == 1)
         for e in (6, 2, 7, 3):
             for z in (0, 1):
                 layer_pass(z, e, z == 0)

@@ -43,6 +43,13 @@ def tile_picked_haar_relu_e_kernel(
         offsets = keep.tile([P, S // LIST_COL], U16, name="offsets")
         band_scales = keep.tile([P, 2 * N], U8, name="band_scales", align_bytes=64)
         nc.gpsimd.memset(band_scales[:].bitcast(I32), 0)
+
+        def load_scales(band, q):
+            nc.sync.dma_start(
+                out=band_scales[32 * q : 32 * q + 4, band * N : (band + 1) * N].bitcast(I32),
+                in_=(w2_scales, w3_scales)[band][0, 4 * q : 4 * q + 4, :].bitcast(I32),
+            )
+
         x_raw = {}
         for pair, loads in enumerate(X_LOADS):
             z, u = divmod(pair, 2)
@@ -55,6 +62,8 @@ def tile_picked_haar_relu_e_kernel(
                 x_raw[pair, i] = (t0, width, on_vector, raw)
                 if pair == 0 and i == 0:
                     nc.sync.dma_start(offsets[:], offs)
+                    for q in range(3):
+                        load_scales(0, q)
                 t0 = t0 + width
         w_raw = []
         for z in range(PASSES):
@@ -62,6 +71,8 @@ def tile_picked_haar_relu_e_kernel(
             rows = w1[z * K_PASS : (z + 1) * K_PASS, :]
             nc.sync.dma_start(out=raw[:], in_=rows.rearrange("(p j) c -> p j c", j=PACK))
             w_raw.append(raw)
+            if z == 0:
+                load_scales(0, 3)
         band_words = []
         for band, words in enumerate((w2_words, w3_words)):
             codes = keep.tile([P, N], U32, name="band_words_%d" % band, align_bytes=64)
@@ -71,12 +82,8 @@ def tile_picked_haar_relu_e_kernel(
             )
             band_words.append(codes)
 
-        for band, scales in enumerate((w2_scales, w3_scales)):
-            for q in range(4):
-                nc.sync.dma_start(
-                    out=band_scales[32 * q : 32 * q + 4, band * N : (band + 1) * N].bitcast(I32),
-                    in_=scales[0, 4 * q : 4 * q + 4, :].bitcast(I32),
-                )
+        for q in range(4):
+            load_scales(1, q)
 
         windows = [keep.tile([P, 2 * T], BF16, name="window_%d" % pair, align_bytes=64) for pair in range(4)]
 
@@ -128,6 +135,7 @@ def tile_picked_haar_relu_e_kernel(
             for i, key in enumerate(sets):
                 x_words[key] = words[:, i * GROUP : (i + 1) * GROUP]
                 x_scales[key] = scales[:, i * GROUP : (i + 1) * GROUP]
+            return words, scales
 
         early = [[(0, 2), (0, 0)], [(1, 0), (1, 2)]]
         late = [[(z, g) for g in ORDER[2:]] for z in range(PASSES)]
@@ -135,7 +143,7 @@ def tile_picked_haar_relu_e_kernel(
             cast(pair, 0)
             for g in ORDER:
                 gather(pair, picked[0, g][:, pair, :], g * GROUP, GROUP)
-        quantise_x(early[0], weave(early[0], "woven_early_0"), "x_words_early_0")
+        early_words = quantise_x(early[0], weave(early[0], "woven_early_0"), "x_words_early_0")
         cast(2, 0)
         gather(2, picked_last[:, 0, :], 0, S)
         for i in range(len(X_LOADS[3])):
@@ -264,8 +272,19 @@ def tile_picked_haar_relu_e_kernel(
         rounded = rounded + round_w1(1, slice(2, PACK), [(slice(0, W_LAST_SCALAR), False), (slice(W_LAST_SCALAR, P), True)])
         quantise_w1(1, rounded)
         quantise_x(late[0], woven_late, "w_bf16_1_2")
-        quantise_x(late[1], weave(late[1], "w_bf16_0_0"), "x_words_late_1")
+        quantise_x(late[1], weave(late[1], "w_raw_1"), "x_words_late_1")
 
+        unread = psum.tile([P, 2 * GROUP], F32, name="unread", tag="bank_3")
+        for i in range(5):
+            nc.tensor.matmul_mx(
+                out=unread[:],
+                lhsT=x_words[0, 2][:, :P].bitcast(FP8X4),
+                lhsT_scale=band_scales[:, :P],
+                rhs=early_words[0][:].bitcast(FP8X4),
+                rhs_scale=early_words[1][:],
+                start=True,
+                stop=True,
+            )
         for e in (4, 0, 5):
             for z in (0, 1):
                 layer_pass(z, e, z == 0)

@@ -92,8 +92,8 @@ def tile_picked_haar_relu_e_kernel(
             for lo, hi, vector in ((0, on_vector, True), (on_vector, width, False)):
                 if hi == lo:
                     continue
-                dst = windows[pair][:, 2 * (t0 + lo) : 2 * (t0 + hi)].rearrange("p (c i e) -> p c e i", i=4, e=2)
-                src = raw[:, :, lo:hi].rearrange("p e (c i) -> p c e i", i=4)
+                dst = windows[pair][:, 2 * (t0 + lo) : 2 * (t0 + hi)].rearrange("p (c e) -> p c e", e=2)
+                src = raw[:, :, lo:hi].rearrange("p e c -> p c e")
                 if vector:
                     nc.vector.tensor_copy(out=dst, in_=src)
                 else:
@@ -125,13 +125,13 @@ def tile_picked_haar_relu_e_kernel(
                     nc.scalar.copy(
                         out=dst.bitcast(U32).rearrange("p (n u) -> p n u", u=2), in_=picked[key].rearrange("p u n -> p n u")
                     )
-            return woven
+            return woven[:]
 
         def quantise_x(sets, woven, tag):
             count = len(sets) * GROUP
             words = keep.tile([P, count], U32, name="x_words_%d_%d" % sets[0], tag=tag, align_bytes=64)
             scales = keep.tile([P, count], U8, name="x_scales_%d_%d" % sets[0], align_bytes=64)
-            nc.vector.quantize_mx(out=words[:].bitcast(FP8X4), scales=scales[:], in_=woven[:])
+            nc.vector.quantize_mx(out=words[:].bitcast(FP8X4), scales=scales[:], in_=woven)
             for i, key in enumerate(sets):
                 x_words[key] = words[:, i * GROUP : (i + 1) * GROUP]
                 x_scales[key] = scales[:, i * GROUP : (i + 1) * GROUP]
@@ -272,7 +272,9 @@ def tile_picked_haar_relu_e_kernel(
         rounded = rounded + round_w1(1, slice(2, PACK), [(slice(0, W_LAST_SCALAR), False), (slice(W_LAST_SCALAR, P), True)])
         quantise_w1(1, rounded)
         quantise_x(late[0], woven_late, "w_bf16_1_2")
-        quantise_x(late[1], weave(late[1], "w_raw_1"), "x_words_late_1")
+        woven_last = weave(late[1], "w_raw_1")
+        for i, key in enumerate(late[1]):
+            quantise_x([key], woven_last[:, i * GROUP * PACK : (i + 1) * GROUP * PACK], "x_words_late_1_%d" % i)
 
         unread = psum.tile([P, 2 * GROUP], F32, name="unread", tag="bank_3")
         for i in range(5):

@@ -22,14 +22,8 @@ PASSES = K // K_PASS
 CHUNK = 128
 GROUP = 256
 LIST_COL = 16
-
-X_LOADS = [
-    [(2048, 1360)],
-    [(2048, 1360)],
-    [(2048, 1216)],
-    [(1024, 0), (1024, 640)],
-]
-W_LAST_SCALAR = 28
+W_SCALAR = ((128, 32), (0, 112))
+X_VECTOR = (512, 512, 512, 512, 256, 256, 256)
 
 
 def tile_picked_haar_relu_e_kernel(
@@ -44,35 +38,29 @@ def tile_picked_haar_relu_e_kernel(
         band_scales = keep.tile([P, 2 * N], U8, name="band_scales", align_bytes=64)
         nc.gpsimd.memset(band_scales[:].bitcast(I32), 0)
 
-        def load_scales(band, q):
-            nc.sync.dma_start(
-                out=band_scales[32 * q : 32 * q + 4, band * N : (band + 1) * N].bitcast(I32),
-                in_=(w2_scales, w3_scales)[band][0, 4 * q : 4 * q + 4, :].bitcast(I32),
-            )
+        one = keep.tile([P, 1], F32, name="one")
+        one_half = keep.tile([P, 1], F32, name="one_half")
+        nc.gpsimd.memset(one[:], 1.0)
+        nc.scalar.activation(out=one_half[:], in_=one[:], func=ACT.Copy, scale=0.5)
 
-        x_raw = {}
-        for pair, loads in enumerate(X_LOADS):
-            z, u = divmod(pair, 2)
+        planes, w_raw = {}, {}
+
+        def load_plane(z, j):
             rows = xT[z * K_PASS : (z + 1) * K_PASS, :].rearrange("(p j) t -> p j t", j=PACK)
-            t0 = 0
-            for i, (width, on_vector) in enumerate(loads):
-                name = "x_raw_%d_%d" % (pair, i)
-                raw = keep.tile([P, 2, width], F32, name=name, tag=name, align_bytes=64)
-                nc.sync.dma_start(out=raw[:], in_=rows[:, 2 * u : 2 * u + 2, t0 : t0 + width])
-                x_raw[pair, i] = (t0, width, on_vector, raw)
-                if pair == 0 and i == 0:
-                    nc.sync.dma_start(offsets[:], offs)
-                    for q in range(3):
-                        load_scales(0, q)
-                t0 = t0 + width
-        w_raw = []
-        for z in range(PASSES):
-            raw = keep.tile([P, PACK, H], F32, name="w_raw_%d" % z, tag="w_raw_%d" % z, align_bytes=64)
+            planes[z, j] = keep.tile([P, T], F32, name="plane_%d_%d" % (z, j), align_bytes=64)
+            nc.sync.dma_start(out=planes[z, j][:], in_=rows[:, j, :])
+
+        def load_w1(z):
+            w_raw[z] = keep.tile([P, PACK, H], F32, name="w_raw_%d" % z, align_bytes=64)
             rows = w1[z * K_PASS : (z + 1) * K_PASS, :]
-            nc.sync.dma_start(out=raw[:], in_=rows.rearrange("(p j) c -> p j c", j=PACK))
-            w_raw.append(raw)
-            if z == 0:
-                load_scales(0, 3)
+            nc.sync.dma_start(out=w_raw[z][:], in_=rows.rearrange("(p j) c -> p j c", j=PACK))
+
+        load_plane(0, 0)
+        nc.sync.dma_start(offsets[:], offs)
+        for z, j in [(0, 1), (0, 2), (0, 3), (1, 0), (1, 1), (1, 2), (1, 3)]:
+            load_plane(z, j)
+        load_w1(0)
+        load_w1(1)
         band_words = []
         for band, words in enumerate((w2_words, w3_words)):
             codes = keep.tile([P, N], U32, name="band_words_%d" % band, align_bytes=64)
@@ -81,96 +69,71 @@ def tile_picked_haar_relu_e_kernel(
                 in_=words[0].rearrange("p n t -> p (n t)").bitcast(I32),
             )
             band_words.append(codes)
-
-        for q in range(4):
-            load_scales(1, q)
-
-        windows = [keep.tile([P, 2 * T], BF16, name="window_%d" % pair, align_bytes=64) for pair in range(4)]
-
-        def cast(pair, i):
-            t0, width, on_vector, raw = x_raw[pair, i]
-            for lo, hi, vector in ((0, on_vector, True), (on_vector, width, False)):
-                if hi == lo:
-                    continue
-                dst = windows[pair][:, 2 * (t0 + lo) : 2 * (t0 + hi)].rearrange("p (c e) -> p c e", e=2)
-                src = raw[:, :, lo:hi].rearrange("p e c -> p c e")
-                if vector:
-                    nc.vector.tensor_copy(out=dst, in_=src)
-                else:
-                    nc.scalar.activation(out=dst, in_=src, func=ACT.Copy)
+        for band, scales in enumerate((w2_scales, w3_scales)):
+            for q in range(4):
+                nc.sync.dma_start(
+                    out=band_scales[32 * q : 32 * q + 4, band * N : (band + 1) * N].bitcast(I32),
+                    in_=scales[0, 4 * q : 4 * q + 4, :].bitcast(I32),
+                )
 
         ORDER = (2, 0, 3, 1)
-        picked = {}
-        picked_last = keep.tile([P, 2, S], U32, name="picked_last", align_bytes=64)
-        for g in ORDER:
-            picked[0, g] = keep.tile([P, 2, GROUP], U32, name="picked_0_%d" % g, align_bytes=64)[:]
-            picked[1, g] = picked_last[:, :, g * GROUP : (g + 1) * GROUP]
-
-        def gather(pair, dst, first, count):
-            piece = offsets[:, first // LIST_COL : (first + count) // LIST_COL]
-            nc.vector.tensor_copy(out=dst, in_=windows[pair][:].bitcast(U32).indirect(piece))
-
-        x_words, x_scales = {}, {}
-
-        def weave(sets, tag, on_vector=False):
-            woven = keep.tile([P, len(sets) * GROUP * PACK], BF16, name="woven_%d_%d" % sets[0], tag=tag, align_bytes=64)
-            for i, key in enumerate(sets):
-                dst = woven[:, i * GROUP * PACK : (i + 1) * GROUP * PACK]
-                if on_vector:
-                    nc.vector.tensor_copy(
-                        out=dst.bitcast(I32).rearrange("p (n u) -> p n u", u=2),
-                        in_=picked[key].bitcast(I32).rearrange("p u n -> p n u"),
-                    )
-                else:
-                    nc.scalar.copy(
-                        out=dst.bitcast(U32).rearrange("p (n u) -> p n u", u=2), in_=picked[key].rearrange("p u n -> p n u")
-                    )
-            return woven[:]
-
-        def quantise_x(sets, woven, tag):
-            count = len(sets) * GROUP
-            words = keep.tile([P, count], U32, name="x_words_%d_%d" % sets[0], tag=tag, align_bytes=64)
-            scales = keep.tile([P, count], U8, name="x_scales_%d_%d" % sets[0], align_bytes=64)
-            nc.vector.quantize_mx(out=words[:].bitcast(FP8X4), scales=scales[:], in_=woven)
-            for i, key in enumerate(sets):
-                x_words[key] = words[:, i * GROUP : (i + 1) * GROUP]
-                x_scales[key] = scales[:, i * GROUP : (i + 1) * GROUP]
-            return words, scales
-
-        early = [[(0, 2), (0, 0)], [(1, 0), (1, 2)]]
-        late = [[(z, g) for g in ORDER[2:]] for z in range(PASSES)]
-        for pair in range(2):
-            cast(pair, 0)
+        picked, woven, x_words, x_scales = {}, {}, {}, {}
+        for z in range(PASSES):
+            picked[z] = keep.tile([P, PACK, S], BF16, name="picked_%d" % z, align_bytes=64)
             for g in ORDER:
-                gather(pair, picked[0, g][:, pair, :], g * GROUP, GROUP)
-        early_words = quantise_x(early[0], weave(early[0], "woven_early_0"), "x_words_early_0")
-        cast(2, 0)
-        gather(2, picked_last[:, 0, :], 0, S)
-        for i in range(len(X_LOADS[3])):
-            cast(3, i)
-        woven_late = weave(late[0], "x_raw_3_1")
+                woven[z, g] = keep.tile([P, GROUP, PACK], BF16, name="woven_%d_%d" % (z, g), align_bytes=64)
+
+        def gather_entries(z, j, lo, hi, on_vector):
+            window = planes[z, j][:].indirect(offsets[:, lo // LIST_COL : hi // LIST_COL])
+            if on_vector:
+                nc.vector.tensor_copy(out=picked[z][:, j, lo:hi], in_=window)
+            else:
+                nc.scalar.activation(out=picked[z][:, j, lo:hi], in_=window, func=ACT.Copy)
+
+        def gather(z, j):
+            if (z, j) == (PASSES - 1, PACK - 1):
+                for g in ORDER:
+                    gather_entries(z, j, g * GROUP, (g + 1) * GROUP, g == 0)
+            else:
+                gather_entries(z, j, 0, X_VECTOR[PACK * z + j], True)
+                gather_entries(z, j, X_VECTOR[PACK * z + j], S, False)
+
+        def weave(z, g, rows):
+            nc.vector.tensor_copy(
+                out=woven[z, g][:, :, rows], in_=picked[z][:, rows, g * GROUP : (g + 1) * GROUP].rearrange("p j n -> p n j")
+            )
+
+        def quantise_x(z, g, tag=None):
+            name = "x_words_%d_%d" % (z, g)
+            x_words[z, g] = keep.tile([P, GROUP], U32, name=name, tag=tag or name, align_bytes=64)
+            x_scales[z, g] = keep.tile([P, GROUP], U8, name="x_scales_%d_%d" % (z, g), align_bytes=64)
+            nc.vector.quantize_mx(
+                out=x_words[z, g][:].bitcast(FP8X4),
+                scales=x_scales[z, g][:],
+                in_=woven[z, g][:].rearrange("p n j -> p (n j)"),
+            )
 
         w_words, w_scales = {}, {}
 
-        def round_w1(z, tiles, parts):
-            name = "w_bf16_%d_%d" % (z, tiles.start)
-            count = tiles.stop - tiles.start
-            grouped = keep.tile([P, count * P * PACK], BF16, name=name, tag=name, align_bytes=64)
-            dst = grouped[:].rearrange("p (t m j) -> p m j t", m=P, j=PACK)
-            src = w_raw[z][:].rearrange("p j (m t) -> p m j t", t=PACK)[:, :, :, tiles]
-            for cols, on_vector in parts:
-                if on_vector:
-                    nc.vector.tensor_scalar(out=dst[:, cols], in0=src[:, cols], scalar1=0.5, scalar2=None, op0=ALU.mult)
-                else:
-                    nc.scalar.activation(out=dst[:, cols], in_=src[:, cols], func=ACT.Copy, scale=0.5)
-            return [grouped[:, i * P * PACK : (i + 1) * P * PACK] for i in range(count)]
-
-        def quantise_w1(z, rounded):
+        def prepare_w1(z):
+            halves = []
+            for half in range(2):
+                name = "w_bf16_%d_%d" % (z, half)
+                grouped = keep.tile([P, 2 * P * PACK], BF16, name=name, tag=name, align_bytes=64)
+                dst = grouped[:].rearrange("p (t m j) -> p m j t", m=P, j=PACK)
+                src = w_raw[z][:].rearrange("p j (m t) -> p m j t", t=PACK)[:, :, :, 2 * half : 2 * half + 2]
+                cut = W_SCALAR[z][half]
+                if cut > 0:
+                    nc.scalar.activation(out=dst[:, :cut], in_=src[:, :cut], func=ACT.Copy, scale=one_half[:])
+                if cut < P:
+                    nc.vector.tensor_scalar(out=dst[:, cut:], in0=src[:, cut:], scalar1=0.5, scalar2=None, op0=ALU.mult)
+                halves.append(grouped)
             w_words[z] = keep.tile([P, H], U32, name="w_words_%d" % z, align_bytes=64)
             w_scales[z] = keep.tile([P, H], U8, name="w_scales_%d" % z, align_bytes=64)
             for t in range(PACK):
                 m = slice(t * P, (t + 1) * P)
-                nc.vector.quantize_mx(out=w_words[z][:, m].bitcast(FP8X4), scales=w_scales[z][:, m], in_=rounded[t])
+                rounded = halves[t // 2][:, (t % 2) * P * PACK : (t % 2 + 1) * P * PACK]
+                nc.vector.quantize_mx(out=w_words[z][:, m].bitcast(FP8X4), scales=w_scales[z][:, m], in_=rounded)
 
         banks = {}
 
@@ -262,39 +225,34 @@ def tile_picked_haar_relu_e_kernel(
                 nc.scalar.activation(out=lower[:], in_=accs[1], func=ACT.Copy)
                 nc.scalar.dma_start(out=out_view[:, 1, cols], in_=lower[:])
 
-        for first in (0, V):
-            gather(3, picked_last[:, 1, first : first + V], first, V)
-        woven_early = [weave([key], "woven_early_1_%d" % key[1], on_vector=True) for key in early[1]]
-        for key, woven in zip(early[1], woven_early):
-            quantise_x([key], woven, "x_words_early_1_%d" % key[1])
-        quantise_w1(0, round_w1(0, slice(0, PACK), [(slice(0, P), False)]))
-        rounded = round_w1(1, slice(0, 2), [(slice(0, P), False)])
-        rounded = rounded + round_w1(1, slice(2, PACK), [(slice(0, W_LAST_SCALAR), False), (slice(W_LAST_SCALAR, P), True)])
-        quantise_w1(1, rounded)
-        quantise_x(late[0], woven_late, "w_bf16_1_2")
-        woven_last = weave(late[1], "w_raw_1")
-        for i, key in enumerate(late[1]):
-            quantise_x([key], woven_last[:, i * GROUP * PACK : (i + 1) * GROUP * PACK], "x_words_late_1_%d" % i)
-
-        unread = psum.tile([P, 2 * GROUP], F32, name="unread", tag="bank_3")
-        for i in range(5):
-            nc.tensor.matmul_mx(
-                out=unread[:],
-                lhsT=x_words[0, 2][:, :P].bitcast(FP8X4),
-                lhsT_scale=band_scales[:, :P],
-                rhs=early_words[0][:].bitcast(FP8X4),
-                rhs_scale=early_words[1][:],
-                start=True,
-                stop=True,
-            )
+        for j in range(PACK):
+            gather(0, j)
+        for g in ORDER:
+            weave(0, g, slice(0, PACK))
+        for g in ORDER:
+            quantise_x(0, g)
+        gather(1, 0)
+        gather(1, 1)
+        for g in ORDER:
+            weave(1, g, slice(0, 2))
+        gather(1, 2)
+        gather(1, 3)
+        for g in ORDER[:2]:
+            weave(1, g, slice(2, PACK))
+        for g in ORDER[:2]:
+            quantise_x(1, g)
+        for g in ORDER[2:]:
+            weave(1, g, slice(2, PACK))
+        prepare_w1(0)
+        prepare_w1(1)
+        quantise_x(1, ORDER[2], "w_bf16_1_1")
+        quantise_x(1, ORDER[3], "w_bf16_1_0")
         for e in (4, 0, 5):
             for z in (0, 1):
                 layer_pass(z, e, z == 0)
-        for z in (1, 0):
-            layer_pass(z, 1, z == 1)
-        for e in (6, 2, 7, 3):
-            for z in (0, 1):
-                layer_pass(z, e, z == 0)
+        for e in (1, 6, 2, 7, 3):
+            for z in (1, 0):
+                layer_pass(z, e, z == 1)
         relu_second(0, parts=2)
         haar(0, 0, parts=2)
         haar(0, 1)

@@ -22,8 +22,15 @@ PASSES = K // K_PASS
 CHUNK = 128
 GROUP = 256
 LIST_COL = 16
-W_SCALAR = ((128, 32), (0, 112))
-X_VECTOR = (512, 512, 512, 512, 256, 256, 256)
+W_SCALAR = ((0, 96), (40, 112))
+X_LOADS = ((0, 0, 2), (0, 2, 2), (1, 0, 2), (1, 2, 1), (1, 3, 1))
+X_RUNS = (
+    ((0, 512), (512, 1024)),
+    ((0, 384), (384, 768), (768, 1024)),
+    ((0, 416), (416, 1024)),
+    ((0, 0), (0, 1024)),
+    ((0, 256), (512, 768), (768, 1024), (256, 512)),
+)
 
 
 def tile_picked_haar_relu_e_kernel(
@@ -45,21 +52,24 @@ def tile_picked_haar_relu_e_kernel(
 
         planes, w_raw = {}, {}
 
-        def load_plane(z, j):
-            rows = xT[z * K_PASS : (z + 1) * K_PASS, :].rearrange("(p j) t -> p j t", j=PACK)
-            planes[z, j] = keep.tile([P, T], F32, name="plane_%d_%d" % (z, j), align_bytes=64)
-            nc.sync.dma_start(out=planes[z, j][:], in_=rows[:, j, :])
+        def load_planes(z, first, count):
+            rows = xT[z * K_PASS : (z + 1) * K_PASS, :].rearrange("(p j) t -> p (j t)", j=PACK)
+            raw = keep.tile([P, count * T], F32, name="planes_%d_%d" % (z, first), align_bytes=64)
+            nc.sync.dma_start(out=raw[:], in_=rows[:, first * T : (first + count) * T])
+            for i in range(count):
+                planes[z, first + i] = raw[:, i * T : (i + 1) * T]
 
         def load_w1(z):
             w_raw[z] = keep.tile([P, PACK, H], F32, name="w_raw_%d" % z, align_bytes=64)
             rows = w1[z * K_PASS : (z + 1) * K_PASS, :]
             nc.sync.dma_start(out=w_raw[z][:], in_=rows.rearrange("(p j) c -> p j c", j=PACK))
 
-        load_plane(0, 0)
+        load_planes(*X_LOADS[0])
         nc.sync.dma_start(offsets[:], offs)
-        for z, j in [(0, 1), (0, 2), (0, 3), (1, 0), (1, 1), (1, 2), (1, 3)]:
-            load_plane(z, j)
+        for load in X_LOADS[1:-1]:
+            load_planes(*load)
         load_w1(0)
+        load_planes(*X_LOADS[-1])
         load_w1(1)
         band_words = []
         for band, words in enumerate((w2_words, w3_words)):
@@ -76,42 +86,44 @@ def tile_picked_haar_relu_e_kernel(
                     in_=scales[0, 4 * q : 4 * q + 4, :].bitcast(I32),
                 )
 
-        ORDER = (2, 0, 3, 1)
         picked, woven, x_words, x_scales = {}, {}, {}, {}
         for z in range(PASSES):
-            picked[z] = keep.tile([P, PACK, S], BF16, name="picked_%d" % z, align_bytes=64)
-            for g in ORDER:
-                woven[z, g] = keep.tile([P, GROUP, PACK], BF16, name="woven_%d_%d" % (z, g), align_bytes=64)
+            picked[z] = keep.tile([P, PACK, S], F32, name="picked_%d" % z, align_bytes=64)
+            woven[z] = keep.tile([P, 2, 2, GROUP, PACK], BF16, name="woven_%d" % z, align_bytes=64)
 
         def gather_entries(z, j, lo, hi, on_vector):
-            window = planes[z, j][:].indirect(offsets[:, lo // LIST_COL : hi // LIST_COL])
+            window = planes[z, j].indirect(offsets[:, lo // LIST_COL : hi // LIST_COL])
             if on_vector:
                 nc.vector.tensor_copy(out=picked[z][:, j, lo:hi], in_=window)
             else:
                 nc.scalar.activation(out=picked[z][:, j, lo:hi], in_=window, func=ACT.Copy)
 
-        def gather(z, j):
-            if (z, j) == (PASSES - 1, PACK - 1):
-                for g in ORDER:
-                    gather_entries(z, j, g * GROUP, (g + 1) * GROUP, g == 0)
+        def gather(load):
+            z, first, count = X_LOADS[load]
+            for run, (lo, hi) in enumerate(X_RUNS[load]):
+                for j in range(first, first + count if hi > lo else first):
+                    gather_entries(z, j, lo, hi, run == 0)
+
+        def weave(z, halves, rows, members=slice(0, 2), on_vector=True):
+            src = picked[z][:].rearrange("p j (d h n) -> p h d n j", d=2, h=2)[:, halves, members, :, rows]
+            dst = woven[z][:, halves, members, :, rows]
+            if on_vector:
+                nc.vector.tensor_copy(out=dst, in_=src)
             else:
-                gather_entries(z, j, 0, X_VECTOR[PACK * z + j], True)
-                gather_entries(z, j, X_VECTOR[PACK * z + j], S, False)
+                nc.scalar.activation(out=dst, in_=src, func=ACT.Copy)
 
-        def weave(z, g, rows):
-            nc.vector.tensor_copy(
-                out=woven[z, g][:, :, rows], in_=picked[z][:, rows, g * GROUP : (g + 1) * GROUP].rearrange("p j n -> p n j")
-            )
-
-        def quantise_x(z, g, tag=None):
-            name = "x_words_%d_%d" % (z, g)
-            x_words[z, g] = keep.tile([P, GROUP], U32, name=name, tag=tag or name, align_bytes=64)
-            x_scales[z, g] = keep.tile([P, GROUP], U8, name="x_scales_%d_%d" % (z, g), align_bytes=64)
+        def quantise_x(z, half, tag=None):
+            name = "x_words_%d_%d" % (z, half)
+            words = keep.tile([P, 2 * GROUP], U32, name=name, tag=tag or name, align_bytes=64)
+            scales = keep.tile([P, 2 * GROUP], U8, name="x_scales_%d_%d" % (z, half), align_bytes=64)
             nc.vector.quantize_mx(
-                out=x_words[z, g][:].bitcast(FP8X4),
-                scales=x_scales[z, g][:],
-                in_=woven[z, g][:].rearrange("p n j -> p (n j)"),
+                out=words[:].bitcast(FP8X4),
+                scales=scales[:],
+                in_=woven[z][:, half].rearrange("p d n j -> p (d n j)"),
             )
+            for n, g in enumerate((half, 2 + half)):
+                x_words[z, g] = words[:, n * GROUP : (n + 1) * GROUP]
+                x_scales[z, g] = scales[:, n * GROUP : (n + 1) * GROUP]
 
         w_words, w_scales = {}, {}
 
@@ -225,34 +237,30 @@ def tile_picked_haar_relu_e_kernel(
                 nc.scalar.activation(out=lower[:], in_=accs[1], func=ACT.Copy)
                 nc.scalar.dma_start(out=out_view[:, 1, cols], in_=lower[:])
 
-        for j in range(PACK):
-            gather(0, j)
-        for g in ORDER:
-            weave(0, g, slice(0, PACK))
-        for g in ORDER:
-            quantise_x(0, g)
-        gather(1, 0)
-        gather(1, 1)
-        for g in ORDER:
-            weave(1, g, slice(0, 2))
-        gather(1, 2)
-        gather(1, 3)
-        for g in ORDER[:2]:
-            weave(1, g, slice(2, PACK))
-        for g in ORDER[:2]:
-            quantise_x(1, g)
-        for g in ORDER[2:]:
-            weave(1, g, slice(2, PACK))
+        gather(0)
+        weave(0, slice(0, 2), slice(0, 2))
+        gather(1)
+        weave(0, slice(0, 1), slice(2, PACK))
+        weave(0, slice(1, 2), slice(2, PACK), slice(0, 1))
+        weave(0, slice(1, 2), slice(2, PACK), slice(1, 2), on_vector=False)
+        for half in range(2):
+            quantise_x(0, half)
+        gather(2)
+        gather(3)
+        weave(1, slice(0, 2), slice(0, 2))
         prepare_w1(0)
+        for e in (4, 0, 5, 1, 6, 2, 7, 3):
+            layer_pass(0, e, True)
+        gather(4)
+        weave(1, slice(0, 1), slice(2, PACK), slice(1, 2))
+        weave(1, slice(0, 1), slice(2, PACK), slice(0, 1))
+        weave(1, slice(1, 2), slice(2, PACK), slice(1, 2))
+        quantise_x(1, 0)
+        weave(1, slice(1, 2), slice(2, PACK), slice(0, 1))
         prepare_w1(1)
-        quantise_x(1, ORDER[2], "w_bf16_1_1")
-        quantise_x(1, ORDER[3], "w_bf16_1_0")
-        for e in (4, 0, 5):
-            for z in (0, 1):
-                layer_pass(z, e, z == 0)
-        for e in (1, 6, 2, 7, 3):
-            for z in (1, 0):
-                layer_pass(z, e, z == 1)
+        quantise_x(1, 1, "w_bf16_1_1")
+        for e in (4, 0, 5, 1, 6, 2, 7, 3):
+            layer_pass(1, e, False)
         relu_second(0, parts=2)
         haar(0, 0, parts=2)
         haar(0, 1)

@@ -22,6 +22,7 @@ PASSES = K // K_PASS
 CHUNK = 128
 GROUP = 256
 LIST_COL = 16
+HIGH_GPSIMD = 56
 W_SCALAR = ((0, 96), (40, 112))
 X_LOADS = ((0, 0, 2), (0, 2, 2), (1, 0, 2), (1, 2, 1), (1, 3, 1))
 X_RUNS = (
@@ -168,7 +169,7 @@ def tile_picked_haar_relu_e_kernel(
                     stop=(not opens and t == tiles[-1]),
                 )
 
-        bands, seconds = {}, {}
+        bands, seconds, firsts = {}, {}, {}
 
         def relu_second(c, parts=1):
             seconds[c] = keep.tile([P, CHUNK, PACK], F32, name="second_%d" % c)
@@ -177,12 +178,20 @@ def tile_picked_haar_relu_e_kernel(
                 cols = slice(lo, lo + CHUNK // parts)
                 nc.scalar.activation(out=seconds[c][:, cols], in_=src[:, cols], func=ACT.Relu)
 
+        def high_on_gpsimd(c):
+            cols = slice(CHUNK - HIGH_GPSIMD, CHUNK)
+            firsts[c] = keep.tile([P, HIGH_GPSIMD, PACK], F32, name="first_%d" % c)
+            nc.scalar.activation(out=firsts[c][:], in_=banks[c][:].rearrange("p t n -> p n t")[:, cols], func=ACT.Relu)
+            bands[c] = keep.tile([P, 2, CHUNK, PACK], BF16, name="bands_%d" % c, tag="bands_%d" % (c % 2), align_bytes=64)
+            nc.gpsimd.tensor_tensor(out=bands[c][:, 1, cols], in0=firsts[c][:], in1=seconds[c][:, cols], op=ALU.subtract)
+
         def haar(c, band, parts=1):
-            if band == 0:
-                bands[c] = keep.tile([P, 2, CHUNK, PACK], BF16, name="bands_%d" % c, align_bytes=64)
+            if c not in bands:
+                bands[c] = keep.tile([P, 2, CHUNK, PACK], BF16, name="bands_%d" % c, tag="bands_0", align_bytes=64)
             src = banks[c][:].rearrange("p t n -> p n t")
-            for lo in range(0, CHUNK, CHUNK // parts):
-                cols = slice(lo, lo + CHUNK // parts)
+            width = CHUNK - HIGH_GPSIMD if band == 1 and c > 0 else CHUNK
+            for lo in range(0, width, width // parts):
+                cols = slice(lo, lo + width // parts)
                 nc.vector.scalar_tensor_tensor(
                     out=bands[c][:, band, cols],
                     in0=src[:, cols],
@@ -265,10 +274,12 @@ def tile_picked_haar_relu_e_kernel(
         haar(0, 0, parts=2)
         haar(0, 1)
         relu_second(1)
+        high_on_gpsimd(1)
         for c in range(1, 4):
-            if c > 1:
-                relu_second(c)
             haar(c, 0)
             finish(c - 1)
+            if c < 3:
+                relu_second(c + 1)
+                high_on_gpsimd(c + 1)
             haar(c, 1)
         finish(3)

@@ -22,15 +22,16 @@ PASSES = K // K_PASS
 CHUNK = 128
 GROUP = 256
 LIST_COL = 16
-HIGH_GPSIMD = 56
-W_SCALAR = ((0, 96), (40, 112))
+WEAVE_SCALAR = 112
+HIGH_GPSIMD = 64
+W_SCALAR = ((0, 112), (16, 108))
 X_LOADS = ((0, 0, 2), (0, 2, 2), (1, 0, 2), (1, 2, 1), (1, 3, 1))
 X_RUNS = (
     ((0, 512), (512, 1024)),
     ((0, 384), (384, 768), (768, 1024)),
     ((0, 416), (416, 1024)),
-    ((0, 0), (0, 1024)),
-    ((0, 256), (512, 768), (768, 1024), (256, 512)),
+    ((0, 0), (0, 256), (256, 1024)),
+    ((0, 0), (512, 768), (768, 1024), (256, 512)),
 )
 
 
@@ -65,9 +66,8 @@ def tile_picked_haar_relu_e_kernel(
             rows = w1[z * K_PASS : (z + 1) * K_PASS, :]
             nc.sync.dma_start(out=w_raw[z][:], in_=rows.rearrange("(p j) c -> p j c", j=PACK))
 
-        load_planes(*X_LOADS[0])
         nc.sync.dma_start(offsets[:], offs)
-        for load in X_LOADS[1:-1]:
+        for load in X_LOADS[:-1]:
             load_planes(*load)
         load_w1(0)
         load_planes(*X_LOADS[-1])
@@ -105,9 +105,9 @@ def tile_picked_haar_relu_e_kernel(
                 for j in range(first, first + count if hi > lo else first):
                     gather_entries(z, j, lo, hi, run == 0)
 
-        def weave(z, halves, rows, members=slice(0, 2), on_vector=True):
-            src = picked[z][:].rearrange("p j (d h n) -> p h d n j", d=2, h=2)[:, halves, members, :, rows]
-            dst = woven[z][:, halves, members, :, rows]
+        def weave(z, halves, rows, members=slice(0, 2), on_vector=True, cols=slice(0, GROUP)):
+            src = picked[z][:].rearrange("p j (d h n) -> p h d n j", d=2, h=2)[:, halves, members, cols, rows]
+            dst = woven[z][:, halves, members, cols, rows]
             if on_vector:
                 nc.vector.tensor_copy(out=dst, in_=src)
             else:
@@ -257,15 +257,19 @@ def tile_picked_haar_relu_e_kernel(
         gather(2)
         gather(3)
         weave(1, slice(0, 2), slice(0, 2))
+        weave(1, slice(0, 1), slice(2, 3), slice(0, 1))
         prepare_w1(0)
         for e in (4, 0, 5, 1, 6, 2, 7, 3):
             layer_pass(0, e, True)
         gather(4)
+        nc.vector.tensor_copy(
+            out=woven[1][:, 0, 0, :, 3], in_=planes[1, 3].indirect(offsets[:, : GROUP // LIST_COL])
+        )
         weave(1, slice(0, 1), slice(2, PACK), slice(1, 2))
-        weave(1, slice(0, 1), slice(2, PACK), slice(0, 1))
         weave(1, slice(1, 2), slice(2, PACK), slice(1, 2))
         quantise_x(1, 0)
-        weave(1, slice(1, 2), slice(2, PACK), slice(0, 1))
+        weave(1, slice(1, 2), slice(2, PACK), slice(0, 1), cols=slice(0, GROUP - WEAVE_SCALAR))
+        weave(1, slice(1, 2), slice(2, PACK), slice(0, 1), on_vector=False, cols=slice(GROUP - WEAVE_SCALAR, GROUP))
         prepare_w1(1)
         quantise_x(1, 1, "w_bf16_1_1")
         for e in (4, 0, 5, 1, 6, 2, 7, 3):

@@ -66,8 +66,9 @@ def tile_picked_haar_relu_e_kernel(
             rows = w1[z * K_PASS : (z + 1) * K_PASS, :]
             nc.sync.dma_start(out=w_raw[z][:], in_=rows.rearrange("(p j) c -> p j c", j=PACK))
 
+        load_planes(*X_LOADS[0])
         nc.sync.dma_start(offsets[:], offs)
-        for load in X_LOADS[:-1]:
+        for load in X_LOADS[1:-1]:
             load_planes(*load)
         load_w1(0)
         load_planes(*X_LOADS[-1])

@@ -22,9 +22,8 @@ PASSES = K // K_PASS
 CHUNK = 128
 GROUP = 256
 LIST_COL = 16
-WEAVE_SCALAR = 112
-HIGH_GPSIMD = 64
-W_SCALAR = ((0, 112), (16, 108))
+HIGH_GPSIMD = 56
+W_SCALAR = ((0, 96), (0, 120))
 X_LOADS = ((0, 0, 2), (0, 2, 2), (1, 0, 2), (1, 2, 1), (1, 3, 1))
 X_RUNS = (
     ((0, 512), (512, 1024)),
@@ -106,9 +105,9 @@ def tile_picked_haar_relu_e_kernel(
                 for j in range(first, first + count if hi > lo else first):
                     gather_entries(z, j, lo, hi, run == 0)
 
-        def weave(z, halves, rows, members=slice(0, 2), on_vector=True, cols=slice(0, GROUP)):
-            src = picked[z][:].rearrange("p j (d h n) -> p h d n j", d=2, h=2)[:, halves, members, cols, rows]
-            dst = woven[z][:, halves, members, cols, rows]
+        def weave(z, halves, rows, members=slice(0, 2), on_vector=True):
+            src = picked[z][:].rearrange("p j (d h n) -> p h d n j", d=2, h=2)[:, halves, members, :, rows]
+            dst = woven[z][:, halves, members, :, rows]
             if on_vector:
                 nc.vector.tensor_copy(out=dst, in_=src)
             else:
@@ -188,9 +187,9 @@ def tile_picked_haar_relu_e_kernel(
 
         def haar(c, band, parts=1):
             if c not in bands:
-                bands[c] = keep.tile([P, 2, CHUNK, PACK], BF16, name="bands_%d" % c, tag="bands_0", align_bytes=64)
+                bands[c] = keep.tile([P, 2, CHUNK, PACK], BF16, name="bands_%d" % c, tag="bands_%d" % c, align_bytes=64)
             src = banks[c][:].rearrange("p t n -> p n t")
-            width = CHUNK - HIGH_GPSIMD if band == 1 and c > 0 else CHUNK
+            width = CHUNK - HIGH_GPSIMD if band == 1 and c > 1 else CHUNK
             for lo in range(0, width, width // parts):
                 cols = slice(lo, lo + width // parts)
                 nc.vector.scalar_tensor_tensor(
@@ -269,8 +268,7 @@ def tile_picked_haar_relu_e_kernel(
         weave(1, slice(0, 1), slice(2, PACK), slice(1, 2))
         weave(1, slice(1, 2), slice(2, PACK), slice(1, 2))
         quantise_x(1, 0)
-        weave(1, slice(1, 2), slice(2, PACK), slice(0, 1), cols=slice(0, GROUP - WEAVE_SCALAR))
-        weave(1, slice(1, 2), slice(2, PACK), slice(0, 1), on_vector=False, cols=slice(GROUP - WEAVE_SCALAR, GROUP))
+        weave(1, slice(1, 2), slice(2, PACK), slice(0, 1))
         prepare_w1(1)
         quantise_x(1, 1, "w_bf16_1_1")
         for e in (4, 0, 5, 1, 6, 2, 7, 3):
@@ -279,7 +277,6 @@ def tile_picked_haar_relu_e_kernel(
         haar(0, 0, parts=2)
         haar(0, 1)
         relu_second(1)
-        high_on_gpsimd(1)
         for c in range(1, 4):
             haar(c, 0)
             finish(c - 1)

@@ -22,7 +22,7 @@ PASSES = K // K_PASS
 CHUNK = 128
 GROUP = 256
 LIST_COL = 16
-HIGH_GPSIMD = 56
+HIGH_GPSIMD = (0, 0, 96, 48)
 W_SCALAR = ((0, 96), (0, 120))
 X_LOADS = ((0, 0, 2), (0, 2, 2), (1, 0, 2), (1, 2, 1), (1, 3, 1))
 X_RUNS = (
@@ -169,37 +169,35 @@ def tile_picked_haar_relu_e_kernel(
                     stop=(not opens and t == tiles[-1]),
                 )
 
-        bands, seconds, firsts = {}, {}, {}
+        bands, seconds = {}, {}
 
-        def relu_second(c, parts=1):
-            seconds[c] = keep.tile([P, CHUNK, PACK], F32, name="second_%d" % c)
+        def relu_second(c, runs, tags=None):
             src = banks[4 + c][:].rearrange("p t n -> p n t")
-            for lo in range(0, CHUNK, CHUNK // parts):
-                cols = slice(lo, lo + CHUNK // parts)
-                nc.scalar.activation(out=seconds[c][:, cols], in_=src[:, cols], func=ACT.Relu)
+            for i, (lo, hi) in enumerate(runs):
+                name = "second_%d_%d" % (c, lo)
+                tag = tags[i] if tags else name
+                seconds[c, lo] = keep.tile([P, hi - lo, PACK], F32, name=name, tag=tag, align_bytes=64)
+                nc.scalar.activation(out=seconds[c, lo][:], in_=src[:, lo:hi], func=ACT.Relu)
+
+        def open_bands(c, tag=None):
+            name = "bands_%d" % c
+            bands[c] = keep.tile([P, 2, CHUNK, PACK], BF16, name=name, tag=tag or name, align_bytes=64)
 
         def high_on_gpsimd(c):
-            cols = slice(CHUNK - HIGH_GPSIMD, CHUNK)
-            firsts[c] = keep.tile([P, HIGH_GPSIMD, PACK], F32, name="first_%d" % c)
-            nc.scalar.activation(out=firsts[c][:], in_=banks[c][:].rearrange("p t n -> p n t")[:, cols], func=ACT.Relu)
-            bands[c] = keep.tile([P, 2, CHUNK, PACK], BF16, name="bands_%d" % c, tag="bands_%d" % (c % 2), align_bytes=64)
-            nc.gpsimd.tensor_tensor(out=bands[c][:, 1, cols], in0=firsts[c][:], in1=seconds[c][:, cols], op=ALU.subtract)
+            width = HIGH_GPSIMD[c]
+            first = keep.tile([P, width, PACK], F32, name="first_%d" % c)
+            nc.scalar.activation(out=first[:], in_=banks[c][:].rearrange("p t n -> p n t")[:, :width], func=ACT.Relu)
+            nc.gpsimd.tensor_tensor(out=bands[c][:, 1, :width], in0=first[:], in1=seconds[c, 0][:, :width], op=ALU.subtract)
 
-        def haar(c, band, parts=1):
-            if c not in bands:
-                bands[c] = keep.tile([P, 2, CHUNK, PACK], BF16, name="bands_%d" % c, tag="bands_%d" % c, align_bytes=64)
-            src = banks[c][:].rearrange("p t n -> p n t")
-            width = CHUNK - HIGH_GPSIMD if band == 1 and c > 1 else CHUNK
-            for lo in range(0, width, width // parts):
-                cols = slice(lo, lo + width // parts)
-                nc.vector.scalar_tensor_tensor(
-                    out=bands[c][:, band, cols],
-                    in0=src[:, cols],
-                    scalar=0.0,
-                    in1=seconds[c][:, cols],
-                    op0=ALU.max,
-                    op1=(ALU.add, ALU.subtract)[band],
-                )
+        def haar(c, band, lo, hi, at):
+            nc.vector.scalar_tensor_tensor(
+                out=bands[c][:, band, lo:hi],
+                in0=banks[c][:].rearrange("p t n -> p n t")[:, lo:hi],
+                scalar=0.0,
+                in1=seconds[c, at][:, lo - at : hi - at],
+                op0=ALU.max,
+                op1=(ALU.add, ALU.subtract)[band],
+            )
 
         out_view = out.rearrange("(h m) v -> m h v", m=P)
 
@@ -273,15 +271,32 @@ def tile_picked_haar_relu_e_kernel(
         quantise_x(1, 1, "w_bf16_1_1")
         for e in (4, 0, 5, 1, 6, 2, 7, 3):
             layer_pass(1, e, False)
-        relu_second(0, parts=2)
-        haar(0, 0, parts=2)
-        haar(0, 1)
-        relu_second(1)
-        for c in range(1, 4):
-            haar(c, 0)
-            finish(c - 1)
-            if c < 3:
-                relu_second(c + 1)
-                high_on_gpsimd(c + 1)
-            haar(c, 1)
+        half, cut = CHUNK // 2, HIGH_GPSIMD[2]
+        first_second = keep.tile([P, CHUNK, PACK], F32, name="second_0")
+        seconds[0, 0] = first_second
+        open_bands(0)
+        for lo in (0, half):
+            src = banks[4][:].rearrange("p t n -> p n t")[:, lo : lo + half]
+            nc.scalar.activation(out=first_second[:, lo : lo + half], in_=src, func=ACT.Relu)
+        haar(0, 0, 0, half, 0)
+        haar(0, 0, half, CHUNK, 0)
+        haar(0, 1, 0, CHUNK, 0)
+        relu_second(1, [(0, CHUNK)])
+        open_bands(1)
+        haar(1, 0, 0, CHUNK, 0)
+        finish(0)
+        relu_second(2, [(0, cut), (cut, CHUNK)], ["shared", "second_2_rest"])
+        open_bands(2)
+        high_on_gpsimd(2)
+        haar(1, 1, 0, CHUNK, 0)
+        haar(2, 0, cut, CHUNK, cut)
+        haar(2, 0, 0, cut, 0)
+        finish(1)
+        relu_second(3, [(0, CHUNK)])
+        open_bands(3, "shared")
+        high_on_gpsimd(3)
+        haar(2, 1, cut, CHUNK, cut)
+        haar(3, 0, 0, CHUNK, 0)
+        finish(2)
+        haar(3, 1, HIGH_GPSIMD[3], CHUNK, 0)
         finish(3)

@@ -21,9 +21,10 @@ K_PASS = P * PACK
 PASSES = K // K_PASS
 CHUNK = 128
 GROUP = 256
+HEAD = 48
 LIST_COL = 16
-HIGH_GPSIMD = (0, 0, 96, 48)
-W_SCALAR = ((0, 96), (0, 120))
+HIGH_GPSIMD = (0, 0, 96, 76)
+W_SCALAR = ((0, 96), (16, 80))
 X_LOADS = ((0, 0, 2), (0, 2, 2), (1, 0, 2), (1, 2, 1), (1, 3, 1))
 X_RUNS = (
     ((0, 512), (512, 1024)),
@@ -105,9 +106,9 @@ def tile_picked_haar_relu_e_kernel(
                 for j in range(first, first + count if hi > lo else first):
                     gather_entries(z, j, lo, hi, run == 0)
 
-        def weave(z, halves, rows, members=slice(0, 2), on_vector=True):
-            src = picked[z][:].rearrange("p j (d h n) -> p h d n j", d=2, h=2)[:, halves, members, :, rows]
-            dst = woven[z][:, halves, members, :, rows]
+        def weave(z, halves, rows, members=slice(0, 2), on_vector=True, part=slice(0, GROUP)):
+            src = picked[z][:].rearrange("p j (d h n) -> p h d n j", d=2, h=2)[:, halves, members, part, rows]
+            dst = woven[z][:, halves, members, part, rows]
             if on_vector:
                 nc.vector.tensor_copy(out=dst, in_=src)
             else:
@@ -152,10 +153,10 @@ def tile_picked_haar_relu_e_kernel(
 
         def layer_pass(z, e, opens):
             if opens:
-                banks[e] = psum.tile([P, PACK, CHUNK], F32, name="bank_%d" % e, tag="bank_%d" % e)
+                banks[e] = psum.tile([P, PACK, CHUNK], F32, name="bank_%d" % e, tag="bank_%d" % (6 if e == 3 else e))
             g, cols = e // 2, slice((e % 2) * CHUNK, (e % 2 + 1) * CHUNK)
             tiles = list(range(PACK))
-            if z == 1 and e != 4:
+            if z == 1 and e not in (4, 0):
                 tiles = tiles[::-1]
             for t in tiles:
                 m = slice(t * P, (t + 1) * P)
@@ -206,7 +207,7 @@ def tile_picked_haar_relu_e_kernel(
             scales = keep.tile([P, 2 * CHUNK], U8, name="haar_scales_%d" % c, align_bytes=64)
             both = bands[c][:].rearrange("p b n t -> p (b n t)")
             parts = 2 if c == 3 else 1
-            for i in range(parts):
+            for i in reversed(range(parts)):
                 w = 2 * CHUNK // parts
                 nc.vector.quantize_mx(
                     out=words[:, i * w : (i + 1) * w].bitcast(FP8X4),
@@ -214,12 +215,12 @@ def tile_picked_haar_relu_e_kernel(
                     in_=both[:, i * w * PACK : (i + 1) * w * PACK],
                 )
             if c < 3:
-                acc = psum.tile([P, 2, CHUNK], F32, name="acc_%d" % c, tag="bank_%d" % (4 + c))
+                acc = psum.tile([P, 2, CHUNK], F32, name="acc_%d" % c, tag="bank_%d" % (4, 5, 3)[c])
                 accs = [acc[:, 0, :], acc[:, 1, :]]
                 order = [(0, 0), (0, 1), (1, 0), (1, 1)]
             else:
                 accs = [psum.tile([P, CHUNK], F32, name="acc_3_%d" % h, tag="bank_%d" % (7, 2)[h])[:] for h in range(2)]
-                order = [(0, 0), (1, 0), (0, 1), (1, 1)]
+                order = [(0, 1), (1, 1), (0, 0), (1, 0)]
             for h, band in order:
                 cols = slice(band * CHUNK, (band + 1) * CHUNK)
                 nc.tensor.matmul_mx(
@@ -228,8 +229,8 @@ def tile_picked_haar_relu_e_kernel(
                     lhsT_scale=band_scales[:, band * N + h * P : band * N + (h + 1) * P],
                     rhs=words[:, cols].bitcast(FP8X4),
                     rhs_scale=scales[:, cols],
-                    start=(band == 0),
-                    stop=(band == 1),
+                    start=(band == order[0][1]),
+                    stop=(band != order[0][1]),
                 )
             cols = slice(c * CHUNK, (c + 1) * CHUNK)
             if c < 3:
@@ -257,7 +258,7 @@ def tile_picked_haar_relu_e_kernel(
         weave(1, slice(0, 2), slice(0, 2))
         weave(1, slice(0, 1), slice(2, 3), slice(0, 1))
         prepare_w1(0)
-        for e in (4, 0, 5, 1, 6, 2, 7, 3):
+        for e in (4, 0, 5, 1, 6, 2, 7):
             layer_pass(0, e, True)
         gather(4)
         nc.vector.tensor_copy(
@@ -266,26 +267,29 @@ def tile_picked_haar_relu_e_kernel(
         weave(1, slice(0, 1), slice(2, PACK), slice(1, 2))
         weave(1, slice(1, 2), slice(2, PACK), slice(1, 2))
         quantise_x(1, 0)
-        weave(1, slice(1, 2), slice(2, PACK), slice(0, 1))
+        weave(1, slice(1, 2), slice(2, PACK), slice(0, 1), True, slice(0, CHUNK))
+        weave(1, slice(1, 2), slice(2, PACK), slice(0, 1), False, slice(CHUNK, GROUP))
         prepare_w1(1)
         quantise_x(1, 1, "w_bf16_1_1")
-        for e in (4, 0, 5, 1, 6, 2, 7, 3):
+        for e in (4, 0, 5, 1, 6, 2, 7):
             layer_pass(1, e, False)
-        half, cut = CHUNK // 2, HIGH_GPSIMD[2]
+        cut = HIGH_GPSIMD[2]
         first_second = keep.tile([P, CHUNK, PACK], F32, name="second_0")
         seconds[0, 0] = first_second
         open_bands(0)
-        for lo in (0, half):
-            src = banks[4][:].rearrange("p t n -> p n t")[:, lo : lo + half]
-            nc.scalar.activation(out=first_second[:, lo : lo + half], in_=src, func=ACT.Relu)
-        haar(0, 0, 0, half, 0)
-        haar(0, 0, half, CHUNK, 0)
-        haar(0, 1, 0, CHUNK, 0)
+        for lo, hi in ((0, HEAD), (HEAD, CHUNK)):
+            src = banks[4][:].rearrange("p t n -> p n t")[:, lo:hi]
+            nc.scalar.activation(out=first_second[:, lo:hi], in_=src, func=ACT.Relu)
+        for lo, hi in ((0, HEAD), (HEAD, CHUNK)):
+            haar(0, 0, lo, hi, 0)
+            haar(0, 1, lo, hi, 0)
         relu_second(1, [(0, CHUNK)])
         open_bands(1)
         haar(1, 0, 0, CHUNK, 0)
         finish(0)
         relu_second(2, [(0, cut), (cut, CHUNK)], ["shared", "second_2_rest"])
+        layer_pass(0, 3, True)
+        layer_pass(1, 3, False)
         open_bands(2)
         high_on_gpsimd(2)
         haar(1, 1, 0, CHUNK, 0)
@@ -296,7 +300,7 @@ def tile_picked_haar_relu_e_kernel(
         open_bands(3, "shared")
         high_on_gpsimd(3)
         haar(2, 1, cut, CHUNK, cut)
+        haar(3, 1, HIGH_GPSIMD[3], CHUNK, 0)
         haar(3, 0, 0, CHUNK, 0)
         finish(2)
-        haar(3, 1, HIGH_GPSIMD[3], CHUNK, 0)
         finish(3)

@@ -23,7 +23,7 @@ CHUNK = 128
 GROUP = 256
 HEAD = 48
 LIST_COL = 16
-HIGH_GPSIMD = (0, 0, 96, 76)
+HIGH_GPSIMD = (0, 0, 88, 56)
 W_SCALAR = ((0, 96), (16, 80))
 X_LOADS = ((0, 0, 2), (0, 2, 2), (1, 0, 2), (1, 2, 1), (1, 3, 1))
 X_RUNS = (
@@ -172,55 +172,59 @@ def tile_picked_haar_relu_e_kernel(
 
         bands, seconds = {}, {}
 
-        def relu_second(c, runs, tags=None):
+        def relu_second(c, cut=0):
             src = banks[4 + c][:].rearrange("p t n -> p n t")
-            for i, (lo, hi) in enumerate(runs):
-                name = "second_%d_%d" % (c, lo)
-                tag = tags[i] if tags else name
-                seconds[c, lo] = keep.tile([P, hi - lo, PACK], F32, name=name, tag=tag, align_bytes=64)
-                nc.scalar.activation(out=seconds[c, lo][:], in_=src[:, lo:hi], func=ACT.Relu)
+            seconds[c] = keep.tile([P, CHUNK, PACK], F32, name="second_%d" % c)
+            for lo, hi in ((0, cut), (cut, CHUNK)) if cut else ((0, CHUNK),):
+                nc.scalar.activation(out=seconds[c][:, lo:hi], in_=src[:, lo:hi], func=ACT.Relu)
 
-        def open_bands(c, tag=None):
-            name = "bands_%d" % c
-            bands[c] = keep.tile([P, 2, CHUNK, PACK], BF16, name=name, tag=tag or name, align_bytes=64)
+        def open_bands(c):
+            tag = "bands_%d" % (1 if c == 3 else c)
+            bands[c] = keep.tile([P, 2, CHUNK, PACK], BF16, name="bands_%d" % c, tag=tag, align_bytes=64)
 
         def high_on_gpsimd(c):
             width = HIGH_GPSIMD[c]
-            first = keep.tile([P, width, PACK], F32, name="first_%d" % c)
+            first = keep.tile([P, width, PACK], F32, name="first_%d" % c, tag="first")
             nc.scalar.activation(out=first[:], in_=banks[c][:].rearrange("p t n -> p n t")[:, :width], func=ACT.Relu)
-            nc.gpsimd.tensor_tensor(out=bands[c][:, 1, :width], in0=first[:], in1=seconds[c, 0][:, :width], op=ALU.subtract)
+            nc.gpsimd.tensor_tensor(out=bands[c][:, 1, :width], in0=first[:], in1=seconds[c][:, :width], op=ALU.subtract)
 
-        def haar(c, band, lo, hi, at):
+        def haar(c, band, lo=0, hi=CHUNK):
             nc.vector.scalar_tensor_tensor(
                 out=bands[c][:, band, lo:hi],
                 in0=banks[c][:].rearrange("p t n -> p n t")[:, lo:hi],
                 scalar=0.0,
-                in1=seconds[c, at][:, lo - at : hi - at],
+                in1=seconds[c][:, lo:hi],
                 op0=ALU.max,
                 op1=(ALU.add, ALU.subtract)[band],
             )
 
         out_view = out.rearrange("(h m) v -> m h v", m=P)
 
-        def finish(c):
+        band_codes = {}
+
+        def quantise_bands(c):
             words = keep.tile([P, 2 * CHUNK], U32, name="haar_words_%d" % c, align_bytes=64)
             scales = keep.tile([P, 2 * CHUNK], U8, name="haar_scales_%d" % c, align_bytes=64)
             both = bands[c][:].rearrange("p b n t -> p (b n t)")
             parts = 2 if c == 3 else 1
-            for i in reversed(range(parts)):
+            for i in range(parts):
                 w = 2 * CHUNK // parts
                 nc.vector.quantize_mx(
                     out=words[:, i * w : (i + 1) * w].bitcast(FP8X4),
                     scales=scales[:, i * w : (i + 1) * w],
                     in_=both[:, i * w * PACK : (i + 1) * w * PACK],
                 )
+            band_codes[c] = words, scales
+
+        def finish(c):
+            words, scales = band_codes[c]
             if c < 3:
                 acc = psum.tile([P, 2, CHUNK], F32, name="acc_%d" % c, tag="bank_%d" % (4, 5, 3)[c])
                 accs = [acc[:, 0, :], acc[:, 1, :]]
                 order = [(0, 0), (0, 1), (1, 0), (1, 1)]
             else:
-                accs = [psum.tile([P, CHUNK], F32, name="acc_3_%d" % h, tag="bank_%d" % (7, 2)[h])[:] for h in range(2)]
-                order = [(0, 1), (1, 1), (0, 0), (1, 0)]
+                accs = [psum.tile([P, CHUNK], F32, name="acc_3_%d" % h, tag="bank_%d" % (7, 0)[h])[:] for h in range(2)]
+                order = [(0, 0), (1, 0), (0, 1), (1, 1)]
             for h, band in order:
                 cols = slice(band * CHUNK, (band + 1) * CHUNK)
                 nc.tensor.matmul_mx(
@@ -229,8 +233,8 @@ def tile_picked_haar_relu_e_kernel(
                     lhsT_scale=band_scales[:, band * N + h * P : band * N + (h + 1) * P],
                     rhs=words[:, cols].bitcast(FP8X4),
                     rhs_scale=scales[:, cols],
-                    start=(band == order[0][1]),
-                    stop=(band != order[0][1]),
+                    start=(band == 0),
+                    stop=(band == 1),
                 )
             cols = slice(c * CHUNK, (c + 1) * CHUNK)
             if c < 3:
@@ -273,34 +277,32 @@ def tile_picked_haar_relu_e_kernel(
         quantise_x(1, 1, "w_bf16_1_1")
         for e in (4, 0, 5, 1, 6, 2, 7):
             layer_pass(1, e, False)
-        cut = HIGH_GPSIMD[2]
-        first_second = keep.tile([P, CHUNK, PACK], F32, name="second_0")
-        seconds[0, 0] = first_second
+        relu_second(0, HEAD)
         open_bands(0)
         for lo, hi in ((0, HEAD), (HEAD, CHUNK)):
-            src = banks[4][:].rearrange("p t n -> p n t")[:, lo:hi]
-            nc.scalar.activation(out=first_second[:, lo:hi], in_=src, func=ACT.Relu)
-        for lo, hi in ((0, HEAD), (HEAD, CHUNK)):
-            haar(0, 0, lo, hi, 0)
-            haar(0, 1, lo, hi, 0)
-        relu_second(1, [(0, CHUNK)])
+            haar(0, 0, lo, hi)
+            haar(0, 1, lo, hi)
+        relu_second(1)
         open_bands(1)
-        haar(1, 0, 0, CHUNK, 0)
-        finish(0)
-        relu_second(2, [(0, cut), (cut, CHUNK)], ["shared", "second_2_rest"])
+        haar(1, 0)
+        quantise_bands(0)
+        relu_second(2, HIGH_GPSIMD[2])
         layer_pass(0, 3, True)
         layer_pass(1, 3, False)
         open_bands(2)
         high_on_gpsimd(2)
-        haar(1, 1, 0, CHUNK, 0)
-        haar(2, 0, cut, CHUNK, cut)
-        haar(2, 0, 0, cut, 0)
-        finish(1)
-        relu_second(3, [(0, CHUNK)])
-        open_bands(3, "shared")
+        haar(1, 1)
+        haar(2, 0)
+        haar(2, 1, HIGH_GPSIMD[2])
+        relu_second(3)
+        finish(0)
+        for c in (1, 2):
+            quantise_bands(c)
+        open_bands(3)
         high_on_gpsimd(3)
-        haar(2, 1, cut, CHUNK, cut)
-        haar(3, 1, HIGH_GPSIMD[3], CHUNK, 0)
-        haar(3, 0, 0, CHUNK, 0)
-        finish(2)
+        for c in (1, 2):
+            finish(c)
+        haar(3, 0)
+        haar(3, 1, HIGH_GPSIMD[3])
+        quantise_bands(3)
         finish(3)

@@ -21,10 +21,9 @@ K_PASS = P * PACK
 PASSES = K // K_PASS
 CHUNK = 128
 GROUP = 256
-HEAD = 48
 LIST_COL = 16
-HIGH_GPSIMD = (0, 0, 88, 56)
-W_SCALAR = ((0, 96), (16, 80))
+HIGH_GPSIMD = (0, 0, 96, 56)
+W_SCALAR = ((0, 96), (0, 120))
 X_LOADS = ((0, 0, 2), (0, 2, 2), (1, 0, 2), (1, 2, 1), (1, 3, 1))
 X_RUNS = (
     ((0, 512), (512, 1024)),
@@ -106,9 +105,9 @@ def tile_picked_haar_relu_e_kernel(
                 for j in range(first, first + count if hi > lo else first):
                     gather_entries(z, j, lo, hi, run == 0)
 
-        def weave(z, halves, rows, members=slice(0, 2), on_vector=True, part=slice(0, GROUP)):
-            src = picked[z][:].rearrange("p j (d h n) -> p h d n j", d=2, h=2)[:, halves, members, part, rows]
-            dst = woven[z][:, halves, members, part, rows]
+        def weave(z, halves, rows, members=slice(0, 2), on_vector=True):
+            src = picked[z][:].rearrange("p j (d h n) -> p h d n j", d=2, h=2)[:, halves, members, :, rows]
+            dst = woven[z][:, halves, members, :, rows]
             if on_vector:
                 nc.vector.tensor_copy(out=dst, in_=src)
             else:
@@ -153,10 +152,10 @@ def tile_picked_haar_relu_e_kernel(
 
         def layer_pass(z, e, opens):
             if opens:
-                banks[e] = psum.tile([P, PACK, CHUNK], F32, name="bank_%d" % e, tag="bank_%d" % (6 if e == 3 else e))
+                banks[e] = psum.tile([P, PACK, CHUNK], F32, name="bank_%d" % e, tag="bank_%d" % e)
             g, cols = e // 2, slice((e % 2) * CHUNK, (e % 2 + 1) * CHUNK)
             tiles = list(range(PACK))
-            if z == 1 and e not in (4, 0):
+            if z == 1 and e != 4:
                 tiles = tiles[::-1]
             for t in tiles:
                 m = slice(t * P, (t + 1) * P)
@@ -219,7 +218,7 @@ def tile_picked_haar_relu_e_kernel(
         def finish(c):
             words, scales = band_codes[c]
             if c < 3:
-                acc = psum.tile([P, 2, CHUNK], F32, name="acc_%d" % c, tag="bank_%d" % (4, 5, 3)[c])
+                acc = psum.tile([P, 2, CHUNK], F32, name="acc_%d" % c, tag="bank_%d" % (4 + c))
                 accs = [acc[:, 0, :], acc[:, 1, :]]
                 order = [(0, 0), (0, 1), (1, 0), (1, 1)]
             else:
@@ -262,7 +261,7 @@ def tile_picked_haar_relu_e_kernel(
         weave(1, slice(0, 2), slice(0, 2))
         weave(1, slice(0, 1), slice(2, 3), slice(0, 1))
         prepare_w1(0)
-        for e in (4, 0, 5, 1, 6, 2, 7):
+        for e in (4, 0, 5, 1, 6, 2, 7, 3):
             layer_pass(0, e, True)
         gather(4)
         nc.vector.tensor_copy(
@@ -271,29 +270,27 @@ def tile_picked_haar_relu_e_kernel(
         weave(1, slice(0, 1), slice(2, PACK), slice(1, 2))
         weave(1, slice(1, 2), slice(2, PACK), slice(1, 2))
         quantise_x(1, 0)
-        weave(1, slice(1, 2), slice(2, PACK), slice(0, 1), True, slice(0, CHUNK))
-        weave(1, slice(1, 2), slice(2, PACK), slice(0, 1), False, slice(CHUNK, GROUP))
+        weave(1, slice(1, 2), slice(2, PACK), slice(0, 1))
         prepare_w1(1)
         quantise_x(1, 1, "w_bf16_1_1")
-        for e in (4, 0, 5, 1, 6, 2, 7):
+        for e in (4, 0, 5, 1, 6, 2, 7, 3):
             layer_pass(1, e, False)
-        relu_second(0, HEAD)
+        half = CHUNK // 2
+        relu_second(0, half)
         open_bands(0)
-        for lo, hi in ((0, HEAD), (HEAD, CHUNK)):
-            haar(0, 0, lo, hi)
-            haar(0, 1, lo, hi)
+        for lo in (0, half):
+            haar(0, 0, lo, lo + half)
+        haar(0, 1)
         relu_second(1)
         open_bands(1)
         haar(1, 0)
         quantise_bands(0)
         relu_second(2, HIGH_GPSIMD[2])
-        layer_pass(0, 3, True)
-        layer_pass(1, 3, False)
         open_bands(2)
         high_on_gpsimd(2)
+        haar(2, 1, HIGH_GPSIMD[2])
         haar(1, 1)
         haar(2, 0)
-        haar(2, 1, HIGH_GPSIMD[2])
         relu_second(3)
         finish(0)
         for c in (1, 2):

@@ -21,9 +21,10 @@ K_PASS = P * PACK
 PASSES = K // K_PASS
 CHUNK = 128
 GROUP = 256
+HEAD = 48
 LIST_COL = 16
 HIGH_GPSIMD = (0, 0, 96, 56)
-W_SCALAR = ((0, 96), (0, 120))
+W_SCALAR = ((0, 96), (16, 80))
 X_LOADS = ((0, 0, 2), (0, 2, 2), (1, 0, 2), (1, 2, 1), (1, 3, 1))
 X_RUNS = (
     ((0, 512), (512, 1024)),
@@ -105,9 +106,9 @@ def tile_picked_haar_relu_e_kernel(
                 for j in range(first, first + count if hi > lo else first):
                     gather_entries(z, j, lo, hi, run == 0)
 
-        def weave(z, halves, rows, members=slice(0, 2), on_vector=True):
-            src = picked[z][:].rearrange("p j (d h n) -> p h d n j", d=2, h=2)[:, halves, members, :, rows]
-            dst = woven[z][:, halves, members, :, rows]
+        def weave(z, halves, rows, members=slice(0, 2), on_vector=True, part=slice(0, GROUP)):
+            src = picked[z][:].rearrange("p j (d h n) -> p h d n j", d=2, h=2)[:, halves, members, part, rows]
+            dst = woven[z][:, halves, members, part, rows]
             if on_vector:
                 nc.vector.tensor_copy(out=dst, in_=src)
             else:
@@ -152,10 +153,10 @@ def tile_picked_haar_relu_e_kernel(
 
         def layer_pass(z, e, opens):
             if opens:
-                banks[e] = psum.tile([P, PACK, CHUNK], F32, name="bank_%d" % e, tag="bank_%d" % e)
+                banks[e] = psum.tile([P, PACK, CHUNK], F32, name="bank_%d" % e, tag="bank_%d" % (6 if e == 3 else e))
             g, cols = e // 2, slice((e % 2) * CHUNK, (e % 2 + 1) * CHUNK)
             tiles = list(range(PACK))
-            if z == 1 and e != 4:
+            if z == 1 and e not in (4, 0):
                 tiles = tiles[::-1]
             for t in tiles:
                 m = slice(t * P, (t + 1) * P)
@@ -218,7 +219,7 @@ def tile_picked_haar_relu_e_kernel(
         def finish(c):
             words, scales = band_codes[c]
             if c < 3:
-                acc = psum.tile([P, 2, CHUNK], F32, name="acc_%d" % c, tag="bank_%d" % (4 + c))
+                acc = psum.tile([P, 2, CHUNK], F32, name="acc_%d" % c, tag="bank_%d" % (4, 5, 3)[c])
                 accs = [acc[:, 0, :], acc[:, 1, :]]
                 order = [(0, 0), (0, 1), (1, 0), (1, 1)]
             else:
@@ -261,7 +262,7 @@ def tile_picked_haar_relu_e_kernel(
         weave(1, slice(0, 2), slice(0, 2))
         weave(1, slice(0, 1), slice(2, 3), slice(0, 1))
         prepare_w1(0)
-        for e in (4, 0, 5, 1, 6, 2, 7, 3):
+        for e in (4, 0, 5, 1, 6, 2, 7):
             layer_pass(0, e, True)
         gather(4)
         nc.vector.tensor_copy(
@@ -270,22 +271,24 @@ def tile_picked_haar_relu_e_kernel(
         weave(1, slice(0, 1), slice(2, PACK), slice(1, 2))
         weave(1, slice(1, 2), slice(2, PACK), slice(1, 2))
         quantise_x(1, 0)
-        weave(1, slice(1, 2), slice(2, PACK), slice(0, 1))
+        weave(1, slice(1, 2), slice(2, PACK), slice(0, 1), True, slice(0, CHUNK))
+        weave(1, slice(1, 2), slice(2, PACK), slice(0, 1), False, slice(CHUNK, GROUP))
         prepare_w1(1)
         quantise_x(1, 1, "w_bf16_1_1")
-        for e in (4, 0, 5, 1, 6, 2, 7, 3):
+        for e in (4, 0, 5, 1, 6, 2, 7):
             layer_pass(1, e, False)
-        half = CHUNK // 2
-        relu_second(0, half)
+        relu_second(0, HEAD)
         open_bands(0)
-        for lo in (0, half):
-            haar(0, 0, lo, lo + half)
-        haar(0, 1)
+        for lo, hi in ((0, HEAD), (HEAD, CHUNK)):
+            haar(0, 0, lo, hi)
+            haar(0, 1, lo, hi)
         relu_second(1)
         open_bands(1)
         haar(1, 0)
         quantise_bands(0)
         relu_second(2, HIGH_GPSIMD[2])
+        layer_pass(0, 3, True)
+        layer_pass(1, 3, False)
         open_bands(2)
         high_on_gpsimd(2)
         haar(2, 1, HIGH_GPSIMD[2])

@@ -247,7 +247,7 @@ def tile_picked_haar_relu_e_kernel(
                 nc.vector.tensor_copy(out=upper[:], in_=accs[0])
                 nc.sync.dma_start(out=out_view[:, 0, cols], in_=upper[:])
                 nc.scalar.activation(out=lower[:], in_=accs[1], func=ACT.Copy)
-                nc.scalar.dma_start(out=out_view[:, 1, cols], in_=lower[:])
+                nc.sync.dma_start(out=out_view[:, 1, cols], in_=lower[:])
 
         gather(0)
         weave(0, slice(0, 2), slice(0, 2))

from contextlib import ExitStack

import concourse.mybir as mybir

K, T, S, V, H, N = 1024, 2048, 1024, 512, 512, 256
FLOPS = 2 * K * H * S + 2 * 2 * H * N * V

F32 = mybir.dt.float32
BF16 = mybir.dt.bfloat16
U32 = mybir.dt.uint32
I32 = mybir.dt.int32
U16 = mybir.dt.uint16
U8 = mybir.dt.uint8
FP8X4 = mybir.dt.float8_e4m3fn_x4
ACT = mybir.ActivationFunctionType
ALU = mybir.AluOpType

P = 128
PACK = 4
K_PASS = P * PACK
PASSES = K // K_PASS
CHUNK = 128
GROUP = 256
HEAD = 48
LIST_COL = 16
HIGH_GPSIMD = (0, 0, 96, 56)
W_SCALAR = ((0, 96), (16, 80))
X_LOADS = ((0, 0, 2), (0, 2, 2), (1, 0, 2), (1, 2, 1), (1, 3, 1))
X_RUNS = (
    ((0, 512), (512, 1024)),
    ((0, 384), (384, 768), (768, 1024)),
    ((0, 416), (416, 1024)),
    ((0, 0), (0, 256), (256, 1024)),
    ((0, 0), (512, 768), (768, 1024), (256, 512)),
)


def tile_picked_haar_relu_e_kernel(
    tc, xT, w1, w2_words, w2_scales, w3_words, w3_scales, offs, out
):
    nc = tc.nc
    with ExitStack() as ctx:
        keep = ctx.enter_context(tc.tile_pool(name="keep", bufs=1))
        psum = ctx.enter_context(tc.psum_pool(name="psum", bufs=1))

        offsets = keep.tile([P, S // LIST_COL], U16, name="offsets")
        band_scales = keep.tile([P, 2 * N], U8, name="band_scales", align_bytes=64)
        nc.gpsimd.memset(band_scales[:].bitcast(I32), 0)

        one = keep.tile([P, 1], F32, name="one")
        one_half = keep.tile([P, 1], F32, name="one_half")
        nc.gpsimd.memset(one[:], 1.0)
        nc.scalar.activation(out=one_half[:], in_=one[:], func=ACT.Copy, scale=0.5)

        planes, w_raw = {}, {}

        def load_planes(z, first, count):
            rows = xT[z * K_PASS : (z + 1) * K_PASS, :].rearrange("(p j) t -> p (j t)", j=PACK)
            raw = keep.tile([P, count * T], F32, name="planes_%d_%d" % (z, first), align_bytes=64)
            nc.sync.dma_start(out=raw[:], in_=rows[:, first * T : (first + count) * T])
            for i in range(count):
                planes[z, first + i] = raw[:, i * T : (i + 1) * T]

        def load_w1(z):
            w_raw[z] = keep.tile([P, PACK, H], F32, name="w_raw_%d" % z, align_bytes=64)
            rows = w1[z * K_PASS : (z + 1) * K_PASS, :]
            nc.sync.dma_start(out=w_raw[z][:], in_=rows.rearrange("(p j) c -> p j c", j=PACK))

        load_planes(*X_LOADS[0])
        nc.sync.dma_start(offsets[:], offs)
        for load in X_LOADS[1:-1]:
            load_planes(*load)
        load_w1(0)
        load_planes(*X_LOADS[-1])
        load_w1(1)
        band_words = []
        for band, words in enumerate((w2_words, w3_words)):
            codes = keep.tile([P, N], U32, name="band_words_%d" % band, align_bytes=64)
            nc.sync.dma_start(
                out=codes[:].bitcast(I32),
                in_=words[0].rearrange("p n t -> p (n t)").bitcast(I32),
            )
            band_words.append(codes)
        for band, scales in enumerate((w2_scales, w3_scales)):
            for q in range(4):
                nc.sync.dma_start(
                    out=band_scales[32 * q : 32 * q + 4, band * N : (band + 1) * N].bitcast(I32),
                    in_=scales[0, 4 * q : 4 * q + 4, :].bitcast(I32),
                )

        picked, woven, x_words, x_scales = {}, {}, {}, {}
        for z in range(PASSES):
            picked[z] = keep.tile([P, PACK, S], F32, name="picked_%d" % z, align_bytes=64)
            woven[z] = keep.tile([P, 2, 2, GROUP, PACK], BF16, name="woven_%d" % z, align_bytes=64)

        def gather_entries(z, j, lo, hi, on_vector):
            window = planes[z, j].indirect(offsets[:, lo // LIST_COL : hi // LIST_COL])
            if on_vector:
                nc.vector.tensor_copy(out=picked[z][:, j, lo:hi], in_=window)
            else:
                nc.scalar.activation(out=picked[z][:, j, lo:hi], in_=window, func=ACT.Copy)

        def gather(load):
            z, first, count = X_LOADS[load]
            for run, (lo, hi) in enumerate(X_RUNS[load]):
                for j in range(first, first + count if hi > lo else first):
                    gather_entries(z, j, lo, hi, run == 0)

        def weave(z, halves, rows, members=slice(0, 2), on_vector=True, part=slice(0, GROUP)):
            src = picked[z][:].rearrange("p j (d h n) -> p h d n j", d=2, h=2)[:, halves, members, part, rows]
            dst = woven[z][:, halves, members, part, rows]
            if on_vector:
                nc.vector.tensor_copy(out=dst, in_=src)
            else:
                nc.scalar.activation(out=dst, in_=src, func=ACT.Copy)

        def quantise_x(z, half, tag=None):
            name = "x_words_%d_%d" % (z, half)
            words = keep.tile([P, 2 * GROUP], U32, name=name, tag=tag or name, align_bytes=64)
            scales = keep.tile([P, 2 * GROUP], U8, name="x_scales_%d_%d" % (z, half), align_bytes=64)
            nc.vector.quantize_mx(
                out=words[:].bitcast(FP8X4),
                scales=scales[:],
                in_=woven[z][:, half].rearrange("p d n j -> p (d n j)"),
            )
            for n, g in enumerate((half, 2 + half)):
                x_words[z, g] = words[:, n * GROUP : (n + 1) * GROUP]
                x_scales[z, g] = scales[:, n * GROUP : (n + 1) * GROUP]

        w_words, w_scales = {}, {}

        def prepare_w1(z):
            halves = []
            for half in range(2):
                name = "w_bf16_%d_%d" % (z, half)
                grouped = keep.tile([P, 2 * P * PACK], BF16, name=name, tag=name, align_bytes=64)
                dst = grouped[:].rearrange("p (t m j) -> p m j t", m=P, j=PACK)
                src = w_raw[z][:].rearrange("p j (m t) -> p m j t", t=PACK)[:, :, :, 2 * half : 2 * half + 2]
                cut = W_SCALAR[z][half]
                if cut > 0:
                    nc.scalar.activation(out=dst[:, :cut], in_=src[:, :cut], func=ACT.Copy, scale=one_half[:])
                if cut < P:
                    nc.vector.tensor_scalar(out=dst[:, cut:], in0=src[:, cut:], scalar1=0.5, scalar2=None, op0=ALU.mult)
                halves.append(grouped)
            w_words[z] = keep.tile([P, H], U32, name="w_words_%d" % z, align_bytes=64)
            w_scales[z] = keep.tile([P, H], U8, name="w_scales_%d" % z, align_bytes=64)
            for t in range(PACK):
                m = slice(t * P, (t + 1) * P)
                rounded = halves[t // 2][:, (t % 2) * P * PACK : (t % 2 + 1) * P * PACK]
                nc.vector.quantize_mx(out=w_words[z][:, m].bitcast(FP8X4), scales=w_scales[z][:, m], in_=rounded)

        banks = {}

        def layer_pass(z, e, opens):
            if opens:
                banks[e] = psum.tile([P, PACK, CHUNK], F32, name="bank_%d" % e, tag="bank_%d" % (6 if e == 3 else e))
            g, cols = e // 2, slice((e % 2) * CHUNK, (e % 2 + 1) * CHUNK)
            tiles = list(range(PACK))
            if z == 1 and e not in (4, 0):
                tiles = tiles[::-1]
            for t in tiles:
                m = slice(t * P, (t + 1) * P)
                nc.tensor.matmul_mx(
                    out=banks[e][:, t, :],
                    lhsT=w_words[z][:, m].bitcast(FP8X4),
                    lhsT_scale=w_scales[z][:, m],
                    rhs=x_words[z, g][:, cols].bitcast(FP8X4),
                    rhs_scale=x_scales[z, g][:, cols],
                    start=(opens and t == tiles[0]),
                    stop=(not opens and t == tiles[-1]),
                )

        bands, seconds = {}, {}

        def relu_second(c, cut=0):
            src = banks[4 + c][:].rearrange("p t n -> p n t")
            seconds[c] = keep.tile([P, CHUNK, PACK], F32, name="second_%d" % c)
            for lo, hi in ((0, cut), (cut, CHUNK)) if cut else ((0, CHUNK),):
                nc.scalar.activation(out=seconds[c][:, lo:hi], in_=src[:, lo:hi], func=ACT.Relu)

        def open_bands(c):
            tag = "bands_%d" % (1 if c == 3 else c)
            bands[c] = keep.tile([P, 2, CHUNK, PACK], BF16, name="bands_%d" % c, tag=tag, align_bytes=64)

        def high_on_gpsimd(c):
            width = HIGH_GPSIMD[c]
            first = keep.tile([P, width, PACK], F32, name="first_%d" % c, tag="first")
            nc.scalar.activation(out=first[:], in_=banks[c][:].rearrange("p t n -> p n t")[:, :width], func=ACT.Relu)
            nc.gpsimd.tensor_tensor(out=bands[c][:, 1, :width], in0=first[:], in1=seconds[c][:, :width], op=ALU.subtract)

        def haar(c, band, lo=0, hi=CHUNK):
            nc.vector.scalar_tensor_tensor(
                out=bands[c][:, band, lo:hi],
                in0=banks[c][:].rearrange("p t n -> p n t")[:, lo:hi],
                scalar=0.0,
                in1=seconds[c][:, lo:hi],
                op0=ALU.max,
                op1=(ALU.add, ALU.subtract)[band],
            )

        out_view = out.rearrange("(h m) v -> m h v", m=P)

        band_codes = {}

        def quantise_bands(c):
            words = keep.tile([P, 2 * CHUNK], U32, name="haar_words_%d" % c, align_bytes=64)
            scales = keep.tile([P, 2 * CHUNK], U8, name="haar_scales_%d" % c, align_bytes=64)
            both = bands[c][:].rearrange("p b n t -> p (b n t)")
            parts = 2 if c == 3 else 1
            for i in range(parts):
                w = 2 * CHUNK // parts
                nc.vector.quantize_mx(
                    out=words[:, i * w : (i + 1) * w].bitcast(FP8X4),
                    scales=scales[:, i * w : (i + 1) * w],
                    in_=both[:, i * w * PACK : (i + 1) * w * PACK],
                )
            band_codes[c] = words, scales

        def finish(c):
            words, scales = band_codes[c]
            if c < 3:
                acc = psum.tile([P, 2, CHUNK], F32, name="acc_%d" % c, tag="bank_%d" % (4, 5, 3)[c])
                accs = [acc[:, 0, :], acc[:, 1, :]]
                order = [(0, 0), (0, 1), (1, 0), (1, 1)]
            else:
                accs = [psum.tile([P, CHUNK], F32, name="acc_3_%d" % h, tag="bank_%d" % (7, 0)[h])[:] for h in range(2)]
                order = [(0, 0), (1, 0), (0, 1), (1, 1)]
            for h, band in order:
                cols = slice(band * CHUNK, (band + 1) * CHUNK)
                nc.tensor.matmul_mx(
                    out=accs[h],
                    lhsT=band_words[band][:, h * P : (h + 1) * P].bitcast(FP8X4),
                    lhsT_scale=band_scales[:, band * N + h * P : band * N + (h + 1) * P],
                    rhs=words[:, cols].bitcast(FP8X4),
                    rhs_scale=scales[:, cols],
                    start=(band == 0),
                    stop=(band == 1),
                )
            cols = slice(c * CHUNK, (c + 1) * CHUNK)
            if c < 3:
                result = keep.tile([P, 2, CHUNK], F32, name="result_%d" % c)
                nc.scalar.activation(out=result[:], in_=acc[:], func=ACT.Copy)
                nc.sync.dma_start(out=out_view[:, :, cols], in_=result[:])
            else:
                upper = keep.tile([P, CHUNK], F32, name="result_upper")
                lower = keep.tile([P, CHUNK], F32, name="result_lower")
                nc.vector.tensor_copy(out=upper[:], in_=accs[0])
                nc.sync.dma_start(out=out_view[:, 0, cols], in_=upper[:])
                nc.scalar.activation(out=lower[:], in_=accs[1], func=ACT.Copy)
                nc.sync.dma_start(out=out_view[:, 1, cols], in_=lower[:])

        gather(0)
        weave(0, slice(0, 2), slice(0, 2))
        gather(1)
        weave(0, slice(0, 1), slice(2, PACK))
        weave(0, slice(1, 2), slice(2, PACK), slice(0, 1))
        weave(0, slice(1, 2), slice(2, PACK), slice(1, 2), on_vector=False)
        for half in range(2):
            quantise_x(0, half)
        gather(2)
        gather(3)
        weave(1, slice(0, 2), slice(0, 2))
        weave(1, slice(0, 1), slice(2, 3), slice(0, 1))
        prepare_w1(0)
        for e in (4, 0, 5, 1, 6, 2, 7):
            layer_pass(0, e, True)
        gather(4)
        nc.vector.tensor_copy(
            out=woven[1][:, 0, 0, :, 3], in_=planes[1, 3].indirect(offsets[:, : GROUP // LIST_COL])
        )
        weave(1, slice(0, 1), slice(2, PACK), slice(1, 2))
        weave(1, slice(1, 2), slice(2, PACK), slice(1, 2))
        quantise_x(1, 0)
        weave(1, slice(1, 2), slice(2, PACK), slice(0, 1), True, slice(0, CHUNK))
        weave(1, slice(1, 2), slice(2, PACK), slice(0, 1), False, slice(CHUNK, GROUP))
        prepare_w1(1)
        quantise_x(1, 1, "w_bf16_1_1")
        for e in (4, 0, 5, 1, 6, 2, 7):
            layer_pass(1, e, False)
        relu_second(0, HEAD)
        open_bands(0)
        for lo, hi in ((0, HEAD), (HEAD, CHUNK)):
            haar(0, 0, lo, hi)
            haar(0, 1, lo, hi)
        relu_second(1)
        open_bands(1)
        haar(1, 0)
        quantise_bands(0)
        relu_second(2, HIGH_GPSIMD[2])
        layer_pass(0, 3, True)
        layer_pass(1, 3, False)
        open_bands(2)
        high_on_gpsimd(2)
        haar(2, 1, HIGH_GPSIMD[2])
        haar(1, 1)
        haar(2, 0)
        relu_second(3)
        finish(0)
        for c in (1, 2):
            quantise_bands(c)
        open_bands(3)
        high_on_gpsimd(3)
        for c in (1, 2):
            finish(c)
        haar(3, 0)
        haar(3, 1, HIGH_GPSIMD[3])
        quantise_bands(3)
        finish(3)
